import numpy as np
CORES = [23,119,17,113]
N = 4
T, FF, CAPT = 2048, 32, 2048
def entries(a): return a.T.reshape(-1)
def pack(v, P): return np.ascontiguousarray(np.asarray(v, np.int32).reshape(-1, P).T)
def lists(rng, how):
    w = rng.random(N) ** 2 + 1e-3; c = T // 8 + ((CAPT - N * (T // 8)) * w / w.sum()).astype(np.int64)
    a = rng.permutation(N)
    if how == "few": c = np.zeros(N, np.int64); c[N - 1] = 3; c[int(rng.integers(N - 1))] = 1
    if how == "lone": s = int(rng.integers(CAPT - T + 1)); c = np.zeros(N, np.int64); c[a[0]] = T; c[a[1]] = s; c[a[2]] = CAPT - T - s
    if how == "none": c = np.zeros(N, np.int64)
    if how == "pair": s = 2 * int(rng.integers(512, 767)) + 1; c = np.zeros(N, np.int64); c[a[0]] = s; c[a[1]] = CAPT - s - 1; c[a[2]] = 1
    if how == "zeros": c = np.full(N, 2); c[0] = T - 7 - 2 * int(rng.integers(T // 16))
    K = np.stack([rng.permutation(np.arange(T) < c[r]) for r in range(N)])
    if how == "zeros": K = np.stack([np.r_[True, rng.permutation(np.arange(T - 2) < c[r] - 2), True] for r in range(N)])
    return {"keep": np.stack([pack(k, 16) for k in K])}
def blank(d):
    for r in range(N):
        k = entries(d["keep"][r]); d["x"][r][:, np.nonzero(k)[0][1:-1:4]] = 0; d["x"][r][:, np.nonzero(1 - k)[0][::4]] = 0
def setup_inputs(rng):
    return dict({"x": rng.standard_normal((N, 128, T), dtype=np.float32), "w1": np.repeat((rng.standard_normal((1, 128, FF * 128), dtype=np.float32) / 8), N, axis=0), "w2": np.repeat((rng.standard_normal((1, 128, FF * 128), dtype=np.float32) / 64), N, axis=0)}, **lists(rng, "uniform"))
def setup_inputs_few(rng):
    d = setup_inputs(rng); d.update(lists(rng, "few"))
    for k in ("x",): d[k] = (d[k].astype(np.float32) * 1024.0).astype(d[k].dtype)
    return d
def setup_inputs_lone(rng):
    d = setup_inputs(rng); d.update(lists(rng, "lone"))
    for k in ("x",): d[k] = (d[k].astype(np.float32) * (1 / 1024.0)).astype(d[k].dtype)
    return d
def setup_inputs_none(rng):
    d = setup_inputs(rng); d.update(lists(rng, "none"))
    return d
def setup_inputs_pair(rng):
    d = setup_inputs(rng); d.update(lists(rng, "pair"))
    return d
def setup_inputs_zeros(rng):
    d = setup_inputs(rng); d.update(lists(rng, "zeros"))
    blank(d)
    return d
def check_inputs(x):
    bad = []
    if x["keep"].min() < 0 or x["keep"].max() >= 2: bad.append("keep out of range")
    if int(x["keep"].sum()) > CAPT: bad.append("more than CAPT tokens are kept in all")
    if any((x[k] != x[k][:1]).any() for k in ("w1", "w2")): bad.append("w1 or w2 is not alike on all ranks")
    return bad
def reference(x, w1, w2, keep):
    X, W1, W2 = x.astype(np.float64), w1.astype(np.float64), w2.astype(np.float64)
    Y = X.copy()
    for r in range(N):
        P = np.nonzero(entries(keep[r]) == 1)[0]
        if len(P) == 0: continue
        Y[r][:, P] = sum(W2[r][:, 128 * f:128 * f + 128].T @ np.maximum(W1[r][:, 128 * f:128 * f + 128].T @ X[r][:, P], 0.0) for f in range(FF))
    return {"y": Y.astype(np.float32)}

@@ -1,0 +1,479 @@
+from concourse.bass import DstId, RemoteDMATransfer
+from concourse.mybir import AluOpType, AxisListType, ActivationFunctionType
+
+SIM_CORES = 128
+NT = 2048
+HALF = 64
+X0 = 4
+R0 = X0 + NT
+WIN = R0 + NT
+ZWIN = 8224
+ROUNDS = [6, 6, 4]
+NEV = 130
+
+SCRATCH = {
+    "wt": ("sbuf", [128, 8192], "float32"),
+    "win": ("sbuf", [128, WIN], "float32"),
+    "pk": ("sbuf", [128, NT], "float32"),
+    "yo": ("sbuf", [128, NT], "float32"),
+    "hid": ("sbuf", [128, 5120], "float32"),
+    "zw": ("sbuf", [128, ZWIN], "bfloat16"),
+    "hi": ("sbuf", [128, 256], "bfloat16"),
+    "lo": ("sbuf", [128, 256], "bfloat16"),
+    "hi0": ("sbuf", [128, 256], "bfloat16"),
+    "lo1": ("sbuf", [128, 256], "bfloat16"),
+    "num": ("sbuf", [128, 256], "bfloat16"),
+    "strip": ("sbuf", [128, 144], "bfloat16"),
+    "mk": ("sbuf", [128, 128], "int32"),
+    "mk15": ("sbuf", [128, 128], "int32"),
+    "up": ("sbuf", [128, 128], "float32"),
+    "ones": ("sbuf", [128, 128], "float32"),
+    "same": ("sbuf", [128, 128], "float32"),
+    "fexp": ("sbuf", [128, 128], "float32"),
+    "pcol": ("sbuf", [128, 4], "int32"),
+    "qi": ("sbuf", [128, 4], "int32"),
+    "p4i": ("sbuf", [128, 4], "int32"),
+    "m0": ("sbuf", [128, 4], "float32"),
+    "m1": ("sbuf", [128, 4], "float32"),
+    "q15": ("sbuf", [128, 4], "float32"),
+    "p4": ("sbuf", [128, 4], "float32"),
+    "cnt": ("sbuf", [128, 4], "float32"),
+    "cnta": ("sbuf", [128, 4], "float32"),
+    "gi": ("sbuf", [128, 8], "float32"),
+    "gm": ("sbuf", [128, 8], "float32"),
+    "kp": ("sbuf", [128, 16], "int32"),
+    "kf": ("sbuf", [128, 16], "float32"),
+    "k1": ("sbuf", [128, 16], "float32"),
+    "nk": ("sbuf", [128, 16], "float32"),
+    "nkt": ("sbuf", [128, 16], "float32"),
+    "zr": ("sbuf", [128, 16], "float32"),
+    "tr": ("sbuf", [128, 16], "float32"),
+    "incl": ("sbuf", [128, 16], "float32"),
+    "gk": ("sbuf", [128, 16], "float32"),
+    "t4a": ("sbuf", [128, 16], "float32"),
+    "t4": ("sbuf", [128, 16], "float32"),
+    "offf": ("sbuf", [128, 16], "float32"),
+    "e1": ("sbuf", [128, 16], "float32"),
+    "e2": ("sbuf", [128, 16], "float32"),
+    "e3": ("sbuf", [128, 16], "float32"),
+    "fw": ("sbuf", [128, 16], "float32"),
+    "off16": ("sbuf", [128, 16], "uint16"),
+    "lu": ("sbuf", [128, 128], "uint16"),
+    "fwu": ("sbuf", [128, 128], "uint16"),
+    "land": ("sbuf", [128, 512], "float32"),
+    "t1": ("sbuf", [128, 128], "float32"),
+    "t2": ("sbuf", [128, 128], "float32"),
+    "vt": ("sbuf", [128, 128], "float32"),
+    "ys": ("sbuf", [128, 128], "float32"),
+    "h0": ("psum", [128, 512], "float32"),
+    "h1": ("psum", [128, 512], "float32"),
+    "h2": ("psum", [128, 512], "float32"),
+    "h3": ("psum", [128, 512], "float32"),
+    "yp0": ("psum", [128, 512], "float32"),
+    "yp1": ("psum", [128, 512], "float32"),
+    "pa": ("psum", [128, 512], "float32"),
+    "pb": ("psum", [128, 512], "float32"),
+}
+REMOTE = (["cntin", "sent"] + ["piece%d" % r for r in range(3)]
+          + ["wr%d%d" % (r, s) for r in range(3) for s in range(2)]
+          + ["tok%s%d" % (k, h) for k in "ab" for h in range(2)] + ["res0", "res1"])
+SEMAPHORES = REMOTE + ["e%d" % i for i in range(NEV)]
+
+
+def weight_layout():
+    reg, col, f = {}, 0, 0
+    for r in range(3):
+        for s in range(2):
+            n = ROUNDS[r]
+            reg[(r, s)] = (col, f, n)
+            col += 256 * n
+            f += n
+    return reg
+
+
+def pieces(reg, r, s):
+    col, _, n = reg[(r, s)]
+    w = 256 * n
+    if w % 3 == 0:
+        return [(i, col + i * w // 3, col + (i + 1) * w // 3) for i in range(3)]
+    q = w // 4
+    return [(i, col + k * q, col + (k + 1) * q) for k, i in enumerate([0, 0, 1, 2])]
+
+
+def bits(m):
+    return [i for i in range(16) if (m >> i) & 1]
+
+
+def mk_mask(bl):
+    return sum(1 << i for i in bl)
+
+
+def rank_program(g, core, T, topo):
+    ranks = list(T.cores)
+    chips = []
+    for c in ranks:
+        if topo.chip(c) not in chips:
+            chips.append(topo.chip(c))
+    if topo.chip(core) not in chips:
+        return
+    workers = [c for ch in chips for c in range(SIM_CORES) if topo.chip(c) == ch]
+    me = workers.index(core)
+    rank = T.rank_of(core)
+    chip = topo.chip(core)
+    pair = [c for c in ranks if topo.chip(c) == chip]
+    other_ranks = [c for c in ranks if topo.chip(c) != chip]
+    local = [c for c in workers if topo.chip(c) == chip]
+    helpers = [[c for c in local if topo.die(c) == topo.die(p) and c not in ranks] for p in pair]
+    side = [i for i in range(2) if core == pair[i] or core in helpers[i]][0]
+    reg = weight_layout()
+    A = AluOpType
+    V, S, P, Y = g.vector, g.scalar, g.tensor, g.sync
+    RELU, COPY = ActivationFunctionType.Relu, ActivationFunctionType.Copy
+
+    events = []
+
+    def ev():
+        e = {"s": T.sem["e%d" % len(events)], "n": 0, "q": []}
+        events.append(e)
+        return e
+
+    def on(e, ins, n=1):
+        ins.then_inc(e["s"], n)
+        e["n"] += n
+        return e
+
+    def do(ins, n=1):
+        return on(ev(), ins, n)
+
+    qs = {"V": V, "S": S, "P": P, "Y": Y, "G": g}
+
+    def wait(q, *es):
+        for e in es:
+            if q not in e["q"]:
+                e["q"].append(q)
+                qs[q].wait_ge(e["s"], e["n"])
+
+    waited = {}
+
+    def rwait(q, name, n):
+        if n and (q, name) not in waited:
+            waited[(q, name)] = n
+            qs[q].wait_ge(T.sem[name], n)
+
+    def did(c):
+        a = topo.addr(c)
+        return DstId(rid=a[0], pnc=a[1])
+
+    sent = [0]
+
+    def send(transfers):
+        out = []
+        for src, dst, dests, eng, sem in transfers:
+            out.append(RemoteDMATransfer(srcs=[src], dsts=[dst] * len(dests), dst_ids=[did(c) for c in dests],
+                                         dma_engine_mask=mk_mask(eng), remote_sem=T.sem[sem]))
+            sent[0] += len(eng)
+        g.remote_dma_fused(out, local_sem=T.sem.sent)
+
+    def engines(c):
+        off = bits(topo.mask(c, [d for d in workers if topo.chip(d) != topo.chip(c)][0]))
+        allb = bits(topo.mask(c, [d for d in workers if topo.chip(d) == topo.chip(c) and d != c][0]))
+        return off, [b for b in allb if b not in off], allb
+
+    def results_to(c):
+        off, stay, _ = engines(c)
+        out = []
+        far = [d for d in ranks if topo.chip(d) != topo.chip(c)]
+        k = len(off) // len(far)
+        for i, d in enumerate(far):
+            out.append((d, off[i * k:(i + 1) * k]))
+        near = [d for d in ranks if topo.chip(d) == topo.chip(c) and d != c]
+        for i, d in enumerate(near):
+            out.append((d, stay[i::len(near)]))
+        return out
+
+    off_eng, stay_eng, all_eng = engines(core)
+    is_rank = rank is not None
+    load = {}
+    gather_ev = {}
+
+    def pass_on(r):
+        mine = [p for p in pieces(reg, r, side) if p[0] == helpers[side].index(core)]
+        lo, hi = mine[0][1], mine[-1][2]
+        rwait("G", "piece%d" % r, 4 * len(mine))
+        dests = [c for c in local if c != core and c != pair[side]]
+        dests = sorted(dests, key=lambda c: topo.die(c) == topo.die(core))
+        send([(T.wt[:, lo:hi], T.wt[:, lo:hi], dests, all_eng, "wr%d%d" % (r, side))])
+
+    def need_weights(r, s):
+        name = "wr%d%d" % (r, s)
+        if is_rank:
+            if s == side:
+                wait("P", load[r])
+            else:
+                rwait("P", name, 3 * len(all_eng))
+        else:
+            if s == side:
+                mine = [p for p in pieces(reg, r, side) if p[0] == helpers[side].index(core)]
+                rwait("P", "piece%d" % r, 4 * len(mine))
+                rwait("P", name, 2 * len(all_eng))
+            else:
+                rwait("P", name, 3 * len(all_eng))
+
+    if is_rank:
+        first = core == pair[0]
+        up = chip == chips[0]
+        kev = ev()
+        for gq in range(8):
+            q = Y if gq < 4 else S
+            on(kev, q.dma_start(T.kp[16 * gq:16 * gq + 16, :], T.keep[:, 16 * gq:16 * gq + 16]), 16)
+
+        def load_round(r, qa, qb):
+            col, f, n = reg[(r, side)]
+            e = ev()
+            on(e, qa.dma_start(T.wt[:, col:col + 128 * n], T.w1[:, 128 * f:128 * (f + n)]), 16)
+            on(e, qb.dma_start(T.wt[:, col + 128 * n:col + 256 * n], T.w2[:, 128 * f:128 * (f + n)]), 16)
+            load[r] = e
+
+        load_round(0, Y, S)
+
+        i_mk = do(g.iota(T.mk[:], [[1, 128]], 0, -1))
+        i_p = do(g.iota(T.pcol[:, 0:1], [[1, 1]], 0, 1))
+        if up:
+            i_tr = do(g.iota(T.tr[:], [[1, 16]], 2064, 32, allow_small_or_imprecise_dtypes=True))
+        else:
+            i_tr = do(g.iota(T.tr[:], [[-1, 16]], 6160, -32, allow_small_or_imprecise_dtypes=True))
+        i_lo = do(g.iota(T.lo[:], [[0, 16], [1, 16]], X0, 0, allow_small_or_imprecise_dtypes=True))
+        i_hi = do(g.iota(T.hi[:], [[16, 16], [0, 16]], 0, 16, allow_small_or_imprecise_dtypes=True))
+        i_t4 = do(g.iota(T.t4a[:], [[16, 16]], X0, 16, allow_small_or_imprecise_dtypes=True))
+        i_gi = do(g.iota(T.gi[:], [[1, 8]], 0, 0, allow_small_or_imprecise_dtypes=True))
+
+        v_zr = do(V.memset(T.zr[:], 0.0))
+        if not first:
+            v_ones = do(V.memset(T.ones[:], 1.0))
+        v_zc = do(V.memset(T.win[:, 0:X0], 0.0))
+        v_zw = do(V.memset(T.zw[:, 0:NT], 0.0))
+        wait("V", i_mk)
+        v_up = do(V.tensor_scalar(out=T.up[:], in0=T.mk[:], scalar1=0, scalar2=None, op0=A.is_gt))
+        wait("V", i_p)
+        v_qi = do(V.tensor_scalar(out=T.qi[:, 0:1], in0=T.pcol[:, 0:1], scalar1=15, scalar2=None, op0=A.bitwise_and))
+        wait("V", v_qi)
+        v_m0 = do(V.tensor_scalar(out=T.m0[:, 0:1], in0=T.qi[:, 0:1], scalar1=0, scalar2=None, op0=A.is_equal))
+        v_m1 = do(V.tensor_scalar(out=T.m1[:, 0:1], in0=T.qi[:, 0:1], scalar1=1, scalar2=None, op0=A.is_equal))
+
+        def numbers():
+            wait("V", i_lo, v_m1)
+            e = ev()
+            on(e, V.tensor_scalar(out=T.lo1[:], in0=T.lo[:], scalar1=T.m1[:, 0:1], scalar2=None, op0=A.mult))
+            s = do(V.tensor_scalar(out=T.strip[:], in0=T.lo[:, 0:144], scalar1=X0 + 15, scalar2=None, op0=A.is_equal))
+            wait("V", i_hi, v_m0)
+            on(e, V.tensor_scalar(out=T.hi0[:], in0=T.hi[:], scalar1=T.m0[:, 0:1], scalar2=None, op0=A.mult))
+            wait("V", e)
+            return s, do(V.tensor_tensor(out=T.num[:], in0=T.hi0[:], in1=T.lo1[:], op=A.add))
+
+        if first:
+            v_strip, v_num = numbers()
+        wait("V", kev)
+        v_kf = do(V.tensor_scalar(out=T.kf[:], in0=T.kp[:], scalar1=1 if up else -1, scalar2=None, op0=A.mult))
+        wait("V", v_kf)
+        v_cnt = do(V.tensor_reduce(out=T.cnt[:, 0:1], in_=T.kf[:], axis=AxisListType.X, op=A.add))
+        v_nk = do(V.tensor_scalar(out=T.nk[:], in0=T.kp[:], scalar1=0, scalar2=None, op0=A.is_equal))
+        wait("V", v_zr)
+        v_in = do(V.tensor_tensor_scan(out=T.incl[:], data0=T.kf[:], data1=T.zr[:], initial=-1.0 if up else float(NT),
+                                       op0=A.add, op1=A.add))
+        wait("V", v_nk, i_tr)
+        v_nkt = do(V.tensor_tensor(out=T.nkt[:], in0=T.nk[:], in1=T.tr[:], op=A.mult))
+        wait("V", v_in, v_nkt)
+        v_gk = do(V.tensor_tensor(out=T.gk[:], in0=T.incl[:], in1=T.nkt[:], op=A.add))
+        if not first:
+            v_strip, v_num = numbers()
+
+        if first:
+            wait("G", v_cnt)
+            send([(T.cnt[:, 0:1], T.cnta[:, 0:1], [pair[1]], all_eng[::2], "cntin")])
+            wait("Y", v_cnt)
+        xev = ev()
+        on(xev, Y.dma_start(T.win[:, X0:X0 + NT // 2], T.x[:, 0:NT // 2]), 16)
+        on(xev, Y.dma_start(T.win[:, X0 + NT // 2:R0], T.x[:, NT // 2:NT]), 16)
+        wait("Y", load[0])
+        load_round(1, Y, Y)
+
+        wait("P", v_up, v_cnt)
+        if first:
+            p_base = do(P.matmul(T.pb[:, 0:1], T.up[:], T.cnt[:, 0:1], True, True))
+        else:
+            p_base = ev()
+            on(p_base, P.matmul(T.pb[:, 0:1], T.up[:], T.cnt[:, 0:1], True, False))
+            wait("P", v_ones)
+            rwait("P", "cntin", len(all_eng[::2]))
+            on(p_base, P.matmul(T.pb[:, 0:1], T.ones[:], T.cnta[:, 0:1], False, True))
+        wait("V", v_gk, p_base)
+        v_off = do(V.tensor_scalar(out=T.off16[:], in0=T.gk[:], scalar1=T.pb[:, 0:1], scalar2=None, op0=A.add))
+        wait("V", v_off, v_num, v_zw)
+        v_sc = do(V.tensor_copy(out=T.zw[:, 0:ZWIN].indirect(T.off16[:, 0:16]), in_=T.num[:]))
+        wait("P", v_sc, v_strip)
+        p_l = []
+        for h in range(2):
+            bank = T.pa if h == 0 else T.pb
+            e = ev()
+            for q in range(16):
+                lo = 1024 * h + q
+                on(e, P.matmul(bank[:, 0:64], T.strip[:, 15 - q:143 - q], T.zw[:, lo:lo + 1009:16], q == 0, q == 15))
+            p_l.append(e)
+        for h in range(2):
+            wait("V", p_l[h])
+            v_lu = do(V.tensor_copy(out=T.lu[:, 64 * h:64 * h + 64], in_=(T.pa if h == 0 else T.pb)[:, 0:64]))
+            wait("V", v_lu, xev, v_zc)
+            gather_ev[(h, 0)] = do(V.tensor_copy(out=T.pk[:, 1024 * h:1024 * h + 512],
+                                                 in_=T.win[:, 0:R0].indirect(T.lu[:, 64 * h:64 * h + 32])))
+            wait("S", v_lu, xev, v_zc)
+            gather_ev[(h, 1)] = do(S.activation(out=T.pk[:, 1024 * h + 512:1024 * h + 1024],
+                                                in_=T.win[:, 0:R0].indirect(T.lu[:, 64 * h + 32:64 * h + 64]), func=COPY))
+
+        def share(r):
+            wait("G", load[r])
+            ps = pieces(reg, r, side)
+            e0 = 4 if r == 1 else 0
+            send([(T.wt[:, lo:hi], T.wt[:, lo:hi], [helpers[side][i]], all_eng[e0 + 4 * k:e0 + 4 * k + 4], "piece%d" % r)
+                  for k, (i, lo, hi) in enumerate(ps)])
+
+        def dispatch(h):
+            wait("G", gather_ev[(h, 0)], gather_ev[(h, 1)])
+            near = [c for c in local if c != core]
+            cross = [c for c in near if topo.die(c) != topo.die(core)]
+            same = [c for c in near if topo.die(c) == topo.die(core)]
+            near = [c for i in range(len(cross)) for c in [cross[i]] + same[i:i + 1]]
+            far = [c for c in workers if topo.chip(c) != chip]
+            tr = []
+            for dests, eng, k in ((far, off_eng, "b"), (near, stay_eng, "a")):
+                for c, b in zip(dests, eng):
+                    lo = 1024 * h + HALF * workers.index(c)
+                    to = 128 * rank + HALF * h
+                    tr.append((T.pk[:, lo:lo + HALF], T.land[:, to:to + HALF], [c], [b], "tok%s%d" % (k, h)))
+            send(tr)
+
+        share(0)
+        dispatch(0)
+        share(1)
+        dispatch(1)
+        wait("Y", load[1])
+        load_round(2, Y, Y)
+        share(2)
+
+        v_k1 = do(V.tensor_copy(out=T.k1[:], in_=T.kp[:]))
+        v_q15 = do(V.tensor_scalar(out=T.q15[:, 0:1], in0=T.qi[:, 0:1], scalar1=15, scalar2=None, op0=A.mult))
+        v_of = do(V.tensor_copy(out=T.offf[:], in_=T.off16[:]))
+        v_p4i = do(V.tensor_scalar(out=T.p4i[:, 0:1], in0=T.pcol[:, 0:1], scalar1=4, scalar2=None, op0=A.arith_shift_right))
+        v_mk15 = do(V.tensor_scalar(out=T.mk15[:], in0=T.mk[:], scalar1=15, scalar2=None, op0=A.bitwise_and))
+        wait("V", i_t4, v_q15)
+        v_t4 = do(V.tensor_scalar(out=T.t4[:], in0=T.t4a[:], scalar1=T.q15[:, 0:1], scalar2=None, op0=A.subtract))
+        wait("V", v_p4i)
+        v_p4 = do(V.tensor_copy(out=T.p4[:, 0:1], in_=T.p4i[:, 0:1]))
+        wait("V", v_mk15)
+        v_same = do(V.tensor_scalar(out=T.same[:], in0=T.mk15[:], scalar1=0, scalar2=None, op0=A.is_equal))
+        wait("V", v_of, v_t4)
+        v_e1 = do(V.tensor_tensor(out=T.e1[:], in0=T.offf[:], in1=T.t4[:], op=A.subtract))
+        wait("V", i_gi, v_p4)
+        v_gm = do(V.tensor_scalar(out=T.gm[:], in0=T.gi[:], scalar1=T.p4[:, 0:1], scalar2=None, op0=A.is_equal))
+        wait("V", v_e1)
+        v_e2 = do(V.tensor_scalar(out=T.e2[:], in0=T.e1[:], scalar1=float(R0), scalar2=None, op0=A.add))
+        wait("V", v_e2, v_k1)
+        v_e3 = do(V.tensor_tensor(out=T.e3[:], in0=T.e2[:], in1=T.k1[:], op=A.mult))
+        wait("V", v_e3)
+        v_fw = do(V.tensor_tensor(out=T.fw[:], in0=T.e3[:], in1=T.t4[:], op=A.add))
+        wait("V", v_fw, v_gm)
+        v_fe = ev()
+        for k in range(8):
+            on(v_fe, V.tensor_scalar(out=T.fexp[:, 16 * k:16 * k + 16], in0=T.fw[:], scalar1=T.gm[:, k:k + 1], scalar2=None,
+                                     op0=A.mult))
+        wait("P", v_same, v_fe)
+        p_f = do(P.matmul(T.pa[:, 0:128], T.same[:], T.fexp[:], True, True))
+        wait("V", p_f)
+        v_fwu = do(V.tensor_copy(out=T.fwu[:], in_=T.pa[:, 0:128]))
+    else:
+        for r in range(3):
+            pass_on(r)
+
+    vt_ev = {}
+
+    def tokens(h):
+        hs = slice(HALF * h, HALF * h + HALF)
+        lands = {}
+        for i, c in enumerate(ranks):
+            if c == core:
+                lo = 1024 * h + HALF * me
+                lands[c] = T.pk[:, lo:lo + HALF]
+                wait("V", gather_ev[(h, 0)], gather_ev[(h, 1)])
+            else:
+                lands[c] = T.land[:, 128 * i + HALF * h:128 * i + HALF * h + HALF]
+        rwait("V", "toka%d" % h, len([c for c in pair if c != core]))
+        a = do(V.tensor_tensor(out=T.t1[:, hs], in0=lands[pair[0]], in1=lands[pair[1]], op=A.add))
+        rwait("V", "tokb%d" % h, len(other_ranks))
+        b = do(V.tensor_tensor(out=T.t2[:, hs], in0=lands[other_ranks[0]], in1=lands[other_ranks[1]], op=A.add))
+        wait("V", a, b)
+        vt_ev[h] = do(V.tensor_tensor(out=T.vt[:, hs], in0=T.t1[:, hs], in1=T.t2[:, hs], op=A.add))
+
+    groups = [[(0, 0)], [(0, 1)], [(1, 0)], [(1, 1)], [(2, 0), (2, 1)]]
+    seq = [(0, 0), (0, 1), (1, 0), (1, 1), (0, 2), (0, 3), (0, 4), (1, 2), (1, 3), (1, 4)]
+    steps = [(1, 0), (1, 1), (2, 0), (1, 2), (2, 1), (1, 3), (1, 4), (2, 2), (1, 5), (2, 3), (1, 6), (2, 4), (1, 7),
+             (2, 5), (2, 6), (1, 8), (2, 7), (1, 9), (2, 8), (2, 9)]
+    banks = [T.h0, T.h1, T.h2, T.h3]
+    ybank = [T.yp0, T.yp1]
+    relu_ev, y_ev, out_ev, done = {}, {}, {}, [0, 0]
+
+    def tiles(gr):
+        out = []
+        for rs in groups[gr]:
+            col, _, n = reg[rs]
+            out += [(col + 128 * i, col + 128 * n + 128 * i) for i in range(n)]
+        return out
+
+    tokens(0)
+    tokens(1)
+    y_ev[0], y_ev[1] = ev(), ev()
+    for layer, idx in steps:
+        h, gr = seq[idx]
+        ts = tiles(gr)
+        if layer == 1:
+            wait("P", vt_ev[h])
+            for r, s in groups[gr]:
+                need_weights(r, s)
+            e = ev()
+            for m, (ca, _) in enumerate(ts):
+                on(e, P.matmul(banks[idx % 4][:, HALF * m:HALF * m + HALF], T.wt[:, ca:ca + 128],
+                               T.vt[:, HALF * h:HALF * h + HALF], True, True))
+            wait("S", e)
+            relu_ev[idx] = do(S.activation(out=T.hid[:, 512 * idx:512 * idx + HALF * len(ts)],
+                                           in_=banks[idx % 4][:, 0:HALF * len(ts)], func=RELU))
+        else:
+            wait("P", relu_ev[idx])
+            for m, (_, cb) in enumerate(ts):
+                lo = 512 * idx + HALF * m
+                on(y_ev[h], P.matmul(ybank[h][:, 0:HALF], T.wt[:, cb:cb + 128], T.hid[:, lo:lo + HALF],
+                                     done[h] == 0, done[h] == 31))
+                done[h] += 1
+            if done[h] == 32:
+                at = R0 + 1024 * h + HALF * me
+                src = T.win[:, at:at + HALF] if is_rank else T.ys[:, HALF * h:HALF * h + HALF]
+                wait("V", y_ev[h])
+                out_ev[h] = do(V.tensor_copy(out=src, in_=ybank[h][:, 0:HALF]))
+                wait("G", out_ev[h])
+                send([(src, T.win[:, at:at + HALF], [c], eng, "res%d" % h) for c, eng in results_to(core)])
+
+    if is_rank:
+        for q in ("V", "S"):
+            wait(q, v_fwu, out_ev[0], out_ev[1])
+            for h in range(2):
+                rwait(q, "res%d" % h, sum(len(e) for w in workers if w != core for c, e in results_to(w) if c == core))
+        yev = ev()
+        for k in range(4):
+            lo = 512 * k
+            a = do(V.tensor_copy(out=T.yo[:, lo:lo + 256], in_=T.win[:, 0:WIN].indirect(T.fwu[:, 32 * k:32 * k + 16])))
+            b = do(S.activation(out=T.yo[:, lo + 256:lo + 512],
+                                in_=T.win[:, 0:WIN].indirect(T.fwu[:, 32 * k + 16:32 * k + 32]), func=COPY))
+            wait("Y", a, b)
+            on(yev, Y.dma_start(T.y[:, lo:lo + 512], T.yo[:, lo:lo + 512]), 16)
+        wait("Y", yev)
+    g.wait_ge(T.sem.sent, sent[0])
+    for e in events:
+        if e["n"] and not e["q"]:
+            wait("G", e)

@@ -9,14 +9,17 @@ R0 = X0 + NT
 WIN = R0 + NT
 ZWIN = 8224
 ROUNDS = [6, 6, 4]
+NR = len(ROUNDS)
+EARLY = 2
+HS = 384
 NEV = 130
 
 SCRATCH = {
-    "wt": ("sbuf", [128, 8192], "float32"),
+    "wt": ("sbuf", [128, 4096], "float32"),
     "win": ("sbuf", [128, WIN], "float32"),
     "pk": ("sbuf", [128, NT], "float32"),
     "yo": ("sbuf", [128, NT], "float32"),
-    "hid": ("sbuf", [128, 5120], "float32"),
+    "hid": ("sbuf", [128, 12 * HS], "float32"),
     "zw": ("sbuf", [128, ZWIN], "bfloat16"),
     "hi": ("sbuf", [128, 256], "bfloat16"),
     "lo": ("sbuf", [128, 256], "bfloat16"),
@@ -65,6 +68,9 @@ SCRATCH = {
     "t2": ("sbuf", [128, 128], "float32"),
     "vt": ("sbuf", [128, 128], "float32"),
     "ys": ("sbuf", [128, 128], "float32"),
+    "pv": ("sbuf", [128, 128], "float32"),
+    "pp": ("sbuf", [128, 128], "float32"),
+    "pl": ("sbuf", [128, 128], "float32"),
     "h0": ("psum", [128, 512], "float32"),
     "h1": ("psum", [128, 512], "float32"),
     "h2": ("psum", [128, 512], "float32"),
@@ -74,30 +80,28 @@ SCRATCH = {
     "pa": ("psum", [128, 512], "float32"),
     "pb": ("psum", [128, 512], "float32"),
 }
-REMOTE = (["cntin", "sent"] + ["piece%d" % r for r in range(3)]
-          + ["wr%d%d" % (r, s) for r in range(3) for s in range(2)]
-          + ["tok%s%d" % (k, h) for k in "ab" for h in range(2)] + ["res0", "res1"])
+REMOTE = (["cntin", "sent"] + ["piece%d" % r for r in range(NR)] + ["wr%d" % r for r in range(NR)]
+          + ["%s%d" % (k, h) for k in ("fwd", "par", "toka", "tokb", "res") for h in range(2)] + ["resf0", "resx"])
 SEMAPHORES = REMOTE + ["e%d" % i for i in range(NEV)]
 
 
-def weight_layout():
-    reg, col, f = {}, 0, 0
-    for r in range(3):
-        for s in range(2):
-            n = ROUNDS[r]
-            reg[(r, s)] = (col, f, n)
-            col += 256 * n
-            f += n
+def weight_layout(side):
+    reg, col, f = [], 0, side * sum(ROUNDS)
+    for n in ROUNDS:
+        reg.append((col, f, n))
+        col += 256 * n
+        f += n
     return reg
 
 
-def pieces(reg, r, s):
-    col, _, n = reg[(r, s)]
-    w = 256 * n
-    if w % 3 == 0:
-        return [(i, col + i * w // 3, col + (i + 1) * w // 3) for i in range(3)]
-    q = w // 4
-    return [(i, col + k * q, col + (k + 1) * q) for k, i in enumerate([0, 0, 1, 2])]
+def pieces(reg, r, eng):
+    col, _, n = reg[r]
+    if r < EARLY:
+        to, es = [0, 0, 0, 1, 1, 1, 2, 2], [eng[2 * i:2 * i + 2] for i in range(8)]
+    else:
+        to, es = [0, 0, 1, 2], [eng[12:14], eng[14:16], eng[8:12], eng[4:8]]
+    q = 256 * n // len(to)
+    return [(i, col + k * q, col + (k + 1) * q, es[k]) for k, i in enumerate(to)]
 
 
 def bits(m):
@@ -120,12 +124,15 @@ def rank_program(g, core, T, topo):
     me = workers.index(core)
     rank = T.rank_of(core)
     chip = topo.chip(core)
-    pair = [c for c in ranks if topo.chip(c) == chip]
-    other_ranks = [c for c in ranks if topo.chip(c) != chip]
+    ck = chips.index(chip)
+    pairs = [[c for c in ranks if topo.chip(c) == ch] for ch in chips]
+    pair, other_ranks = pairs[ck], pairs[1 - ck]
     local = [c for c in workers if topo.chip(c) == chip]
     helpers = [[c for c in local if topo.die(c) == topo.die(p) and c not in ranks] for p in pair]
     side = [i for i in range(2) if core == pair[i] or core in helpers[i]][0]
-    reg = weight_layout()
+    mine, theirs = [pair[side]] + helpers[side], [pair[1 - side]] + helpers[1 - side]
+    partner = theirs[mine.index(core)]
+    reg = weight_layout(side)
     A = AluOpType
     V, S, P, Y = g.vector, g.scalar, g.tensor, g.sync
     RELU, COPY = ActivationFunctionType.Relu, ActivationFunctionType.Copy
@@ -179,62 +186,63 @@ def rank_program(g, core, T, topo):
         allb = bits(topo.mask(c, [d for d in workers if topo.chip(d) == topo.chip(c) and d != c][0]))
         return off, [b for b in allb if b not in off], allb
 
-    def results_to(c):
+    def results_to(c, h):
         off, stay, _ = engines(c)
-        out = []
         far = [d for d in ranks if topo.chip(d) != topo.chip(c)]
+        if h == 0:
+            far = [d for d in far if topo.die(d) == topo.die(c)]
         k = len(off) // len(far)
-        for i, d in enumerate(far):
-            out.append((d, off[i * k:(i + 1) * k]))
+        out = [(d, off[i * k:(i + 1) * k], "resf0" if h == 0 else "res1") for i, d in enumerate(far)]
         near = [d for d in ranks if topo.chip(d) == topo.chip(c) and d != c]
-        for i, d in enumerate(near):
-            out.append((d, stay[i::len(near)]))
-        return out
+        return out + [(d, stay[i::len(near)], "res%d" % h) for i, d in enumerate(near)]
 
     off_eng, stay_eng, all_eng = engines(core)
     is_rank = rank is not None
+    fwd_eng = all_eng[0:4] if is_rank else stay_eng
     load = {}
     gather_ev = {}
 
-    def pass_on(r):
-        mine = [p for p in pieces(reg, r, side) if p[0] == helpers[side].index(core)]
-        lo, hi = mine[0][1], mine[-1][2]
-        rwait("G", "piece%d" % r, 4 * len(mine))
-        dests = [c for c in local if c != core and c != pair[side]]
-        dests = sorted(dests, key=lambda c: topo.die(c) == topo.die(core))
-        send([(T.wt[:, lo:hi], T.wt[:, lo:hi], dests, all_eng, "wr%d%d" % (r, side))])
+    def part(r):
+        ps = [p for p in pieces(reg, r, all_eng) if p[0] == helpers[side].index(core)]
+        return ps[0][1], ps[-1][2], sum(len(p[3]) for p in ps)
 
-    def need_weights(r, s):
-        name = "wr%d%d" % (r, s)
+    def pass_on(r):
+        lo, hi, n = part(r)
+        rwait("G", "piece%d" % r, n)
+        send([(T.wt[:, lo:hi], T.wt[:, lo:hi], [c for c in helpers[side] if c != core], all_eng, "wr%d" % r)])
+
+    def need_weights(r):
         if is_rank:
-            if s == side:
-                wait("P", load[r])
-            else:
-                rwait("P", name, 3 * len(all_eng))
+            wait("P", load[r])
         else:
-            if s == side:
-                mine = [p for p in pieces(reg, r, side) if p[0] == helpers[side].index(core)]
-                rwait("P", "piece%d" % r, 4 * len(mine))
-                rwait("P", name, 2 * len(all_eng))
-            else:
-                rwait("P", name, 3 * len(all_eng))
+            rwait("P", "piece%d" % r, part(r)[2])
+            rwait("P", "wr%d" % r, 2 * len(all_eng))
 
     if is_rank:
         first = core == pair[0]
-        up = chip == chips[0]
+        up = ck == 0
         kev = ev()
         for gq in range(8):
             q = Y if gq < 4 else S
             on(kev, q.dma_start(T.kp[16 * gq:16 * gq + 16, :], T.keep[:, 16 * gq:16 * gq + 16]), 16)
 
         def load_round(r, qa, qb):
-            col, f, n = reg[(r, side)]
+            col, f, n = reg[r]
             e = ev()
             on(e, qa.dma_start(T.wt[:, col:col + 128 * n], T.w1[:, 128 * f:128 * (f + n)]), 16)
             on(e, qb.dma_start(T.wt[:, col + 128 * n:col + 256 * n], T.w2[:, 128 * f:128 * (f + n)]), 16)
             load[r] = e
 
-        load_round(0, Y, S)
+        xev = ev()
+
+        def load_x():
+            on(xev, Y.dma_start(T.win[:, X0:X0 + NT // 2], T.x[:, 0:NT // 2]), 16)
+            on(xev, Y.dma_start(T.win[:, X0 + NT // 2:R0], T.x[:, NT // 2:NT]), 16)
+
+        for r in range(EARLY):
+            load_round(r, Y, S)
+        if not first:
+            load_x()
 
         i_mk = do(g.iota(T.mk[:], [[1, 128]], 0, -1))
         i_p = do(g.iota(T.pcol[:, 0:1], [[1, 1]], 0, 1))
@@ -260,18 +268,6 @@ def rank_program(g, core, T, topo):
         v_m0 = do(V.tensor_scalar(out=T.m0[:, 0:1], in0=T.qi[:, 0:1], scalar1=0, scalar2=None, op0=A.is_equal))
         v_m1 = do(V.tensor_scalar(out=T.m1[:, 0:1], in0=T.qi[:, 0:1], scalar1=1, scalar2=None, op0=A.is_equal))
 
-        def numbers():
-            wait("V", i_lo, v_m1)
-            e = ev()
-            on(e, V.tensor_scalar(out=T.lo1[:], in0=T.lo[:], scalar1=T.m1[:, 0:1], scalar2=None, op0=A.mult))
-            s = do(V.tensor_scalar(out=T.strip[:], in0=T.lo[:, 0:144], scalar1=X0 + 15, scalar2=None, op0=A.is_equal))
-            wait("V", i_hi, v_m0)
-            on(e, V.tensor_scalar(out=T.hi0[:], in0=T.hi[:], scalar1=T.m0[:, 0:1], scalar2=None, op0=A.mult))
-            wait("V", e)
-            return s, do(V.tensor_tensor(out=T.num[:], in0=T.hi0[:], in1=T.lo1[:], op=A.add))
-
-        if first:
-            v_strip, v_num = numbers()
         wait("V", kev)
         v_kf = do(V.tensor_scalar(out=T.kf[:], in0=T.kp[:], scalar1=1 if up else -1, scalar2=None, op0=A.mult))
         wait("V", v_kf)
@@ -284,18 +280,20 @@ def rank_program(g, core, T, topo):
         v_nkt = do(V.tensor_tensor(out=T.nkt[:], in0=T.nk[:], in1=T.tr[:], op=A.mult))
         wait("V", v_in, v_nkt)
         v_gk = do(V.tensor_tensor(out=T.gk[:], in0=T.incl[:], in1=T.nkt[:], op=A.add))
-        if not first:
-            v_strip, v_num = numbers()
+        wait("V", i_lo, v_m1)
+        v_lh = ev()
+        on(v_lh, V.tensor_scalar(out=T.lo1[:], in0=T.lo[:], scalar1=T.m1[:, 0:1], scalar2=None, op0=A.mult))
+        v_strip = do(V.tensor_scalar(out=T.strip[:], in0=T.lo[:, 0:144], scalar1=X0 + 15, scalar2=None, op0=A.is_equal))
+        wait("V", i_hi, v_m0)
+        on(v_lh, V.tensor_scalar(out=T.hi0[:], in0=T.hi[:], scalar1=T.m0[:, 0:1], scalar2=None, op0=A.mult))
+        wait("V", v_lh)
+        v_num = do(V.tensor_tensor(out=T.num[:], in0=T.hi0[:], in1=T.lo1[:], op=A.add))
 
         if first:
+            wait("Y", v_cnt)
+            load_x()
             wait("G", v_cnt)
             send([(T.cnt[:, 0:1], T.cnta[:, 0:1], [pair[1]], all_eng[::2], "cntin")])
-            wait("Y", v_cnt)
-        xev = ev()
-        on(xev, Y.dma_start(T.win[:, X0:X0 + NT // 2], T.x[:, 0:NT // 2]), 16)
-        on(xev, Y.dma_start(T.win[:, X0 + NT // 2:R0], T.x[:, NT // 2:NT]), 16)
-        wait("Y", load[0])
-        load_round(1, Y, Y)
 
         wait("P", v_up, v_cnt)
         if first:
@@ -328,20 +326,21 @@ def rank_program(g, core, T, topo):
             wait("S", v_lu, xev, v_zc)
             gather_ev[(h, 1)] = do(S.activation(out=T.pk[:, 1024 * h + 512:1024 * h + 1024],
                                                 in_=T.win[:, 0:R0].indirect(T.lu[:, 64 * h + 32:64 * h + 64]), func=COPY))
+        wait("Y", p_l[0])
+        for r in range(EARLY, NR):
+            load_round(r, Y, Y)
 
         def share(r):
             wait("G", load[r])
-            ps = pieces(reg, r, side)
-            e0 = 4 if r == 1 else 0
-            send([(T.wt[:, lo:hi], T.wt[:, lo:hi], [helpers[side][i]], all_eng[e0 + 4 * k:e0 + 4 * k + 4], "piece%d" % r)
-                  for k, (i, lo, hi) in enumerate(ps)])
+            send([(T.wt[:, lo:hi], T.wt[:, lo:hi], [helpers[side][i]], eng, "piece%d" % r)
+                  for i, lo, hi, eng in pieces(reg, r, all_eng)])
 
         def dispatch(h):
             wait("G", gather_ev[(h, 0)], gather_ev[(h, 1)])
             near = [c for c in local if c != core]
-            cross = [c for c in near if topo.die(c) != topo.die(core)]
+            over = [c for c in near if topo.die(c) != topo.die(core)]
             same = [c for c in near if topo.die(c) == topo.die(core)]
-            near = [c for i in range(len(cross)) for c in [cross[i]] + same[i:i + 1]]
+            near = [c for i in range(len(over)) for c in [over[i]] + same[i:i + 1]]
             far = [c for c in workers if topo.chip(c) != chip]
             tr = []
             for dests, eng, k in ((far, off_eng, "b"), (near, stay_eng, "a")):
@@ -351,14 +350,58 @@ def rank_program(g, core, T, topo):
                     tr.append((T.pk[:, lo:lo + HALF], T.land[:, to:to + HALF], [c], [b], "tok%s%d" % (k, h)))
             send(tr)
 
-        share(0)
+        for r in range(EARLY):
+            share(r)
         dispatch(0)
-        share(1)
         dispatch(1)
-        wait("Y", load[1])
-        load_round(2, Y, Y)
-        share(2)
+        for r in range(EARLY, NR):
+            share(r)
+    else:
+        for r in range(EARLY):
+            pass_on(r)
 
+    vt_ev = {}
+
+    def tokens(h):
+        hs = slice(HALF * h, HALF * h + HALF)
+        lands = {}
+        for i, c in enumerate(ranks):
+            if c == core:
+                lo = 1024 * h + HALF * me
+                lands[c] = T.pk[:, lo:lo + HALF]
+                wait("V", gather_ev[(h, 0)], gather_ev[(h, 1)])
+            else:
+                lands[c] = T.land[:, 128 * i + HALF * h:128 * i + HALF * h + HALF]
+        rwait("V", "toka%d" % h, len([c for c in pair if c != core]))
+        a = do(V.tensor_tensor(out=T.t1[:, hs], in0=lands[pair[0]], in1=lands[pair[1]], op=A.add))
+        rwait("V", "tokb%d" % h, len(other_ranks))
+        b = do(V.tensor_tensor(out=T.t2[:, hs], in0=lands[other_ranks[0]], in1=lands[other_ranks[1]], op=A.add))
+        wait("V", a, b)
+        vt_ev[h] = do(V.tensor_tensor(out=T.vt[:, hs], in0=T.t1[:, hs], in1=T.t2[:, hs], op=A.add))
+
+    seq = [(0, 0, 6), (0, 6, 12), (2, 0, 6), (2, 6, 12), (1, 0, 6), (3, 0, 6), (2, 12, 16), (3, 6, 12), (3, 12, 16),
+           (0, 12, 16), (1, 6, 12), (1, 12, 16)]
+    steps = [(1, 0), (1, 1), (2, 0), (2, 1), (1, 2), (1, 3), (2, 2)]
+    for i in range(4, len(seq)):
+        steps += [(1, i), (2, i - 2)]
+        if seq[i - 1][0] not in [q[0] for q in seq[i:]]:
+            steps.append((2, i - 1))
+    steps += [(2, i) for i in range(len(seq))]
+    steps = [st for i, st in enumerate(steps) if st not in steps[:i]]
+    tiles = []
+    for r, (col, f, n) in enumerate(reg):
+        tiles += [(r, col + 128 * i, col + 128 * (n + i)) for i in range(n)]
+    banks = [T.h0, T.h1, T.h2, T.h3]
+    ybank = [T.yp0, T.yp1, T.pa, T.pb]
+    relu_ev, out_ev, pp_ev, done = {}, {}, {}, [0] * 4
+    y_ev = [ev() for _ in range(4)]
+
+    for h in range(2):
+        tokens(h)
+        wait("G", vt_ev[h])
+        hs = slice(HALF * h, HALF * h + HALF)
+        send([(T.vt[:, hs], T.pv[:, hs], [partner], fwd_eng, "fwd%d" % h)])
+    if is_rank:
         v_k1 = do(V.tensor_copy(out=T.k1[:], in_=T.kp[:]))
         v_q15 = do(V.tensor_scalar(out=T.q15[:, 0:1], in0=T.qi[:, 0:1], scalar1=15, scalar2=None, op0=A.mult))
         v_of = do(V.tensor_copy(out=T.offf[:], in_=T.off16[:]))
@@ -385,85 +428,70 @@ def rank_program(g, core, T, topo):
         for k in range(8):
             on(v_fe, V.tensor_scalar(out=T.fexp[:, 16 * k:16 * k + 16], in0=T.fw[:], scalar1=T.gm[:, k:k + 1], scalar2=None,
                                      op0=A.mult))
-        wait("P", v_same, v_fe)
+    else:
+        for r in range(EARLY, NR):
+            pass_on(r)
+    for layer, idx in steps:
+        st, fa, fb = seq[idx]
+        h = st % 2
+        hs = slice(HALF * h, HALF * h + HALF)
+        tl = tiles[fa:fb]
+        n = len(tl)
+        if layer == 1:
+            if st < 2:
+                wait("P", vt_ev[h])
+            else:
+                rwait("P", "fwd%d" % h, len(all_eng[0:4]) if is_rank else len(stay_eng))
+            for r in sorted(set(t[0] for t in tl)):
+                need_weights(r)
+            e = ev()
+            for m, (_, ca, _) in enumerate(tl):
+                on(e, P.matmul(banks[idx % 4][:, HALF * m:HALF * m + HALF], T.wt[:, ca:ca + 128],
+                               T.vt[:, hs] if st < 2 else T.pv[:, hs], True, True))
+            wait("S", e)
+            relu_ev[idx] = do(S.activation(out=T.hid[:, HS * idx:HS * idx + HALF * n],
+                                           in_=banks[idx % 4][:, 0:HALF * n], func=RELU))
+            continue
+        wait("P", relu_ev[idx])
+        for m, (_, _, cb) in enumerate(tl):
+            lo = HS * idx + HALF * m
+            on(y_ev[st], P.matmul(ybank[st][:, 0:HALF], T.wt[:, cb:cb + 128], T.hid[:, lo:lo + HALF],
+                                  done[st] == 0, done[st] == len(tiles) - 1))
+            done[st] += 1
+        if done[st] < len(tiles):
+            continue
+        wait("V", y_ev[st])
+        if st >= 2:
+            pp_ev[h] = do(V.tensor_copy(out=T.pp[:, hs], in_=ybank[st][:, 0:HALF]))
+            wait("G", pp_ev[h])
+            send([(T.pp[:, hs], T.pl[:, hs], [partner], all_eng, "par%d" % h)])
+        else:
+            at = R0 + 1024 * h + HALF * me
+            src = T.win[:, at:at + HALF] if is_rank else T.ys[:, hs]
+            rwait("V", "par%d" % h, len(all_eng))
+            out_ev[h] = do(V.tensor_tensor(out=src, in0=ybank[st][:, 0:HALF], in1=T.pl[:, hs], op=A.add))
+            wait("G", out_ev[h])
+            send([(src, T.win[:, at:at + HALF], [c], eng, sem) for c, eng, sem in results_to(core, h)])
+
+    if is_rank:
+        wait("P", v_same, v_fe, pp_ev[0])
         p_f = do(P.matmul(T.pa[:, 0:128], T.same[:], T.fexp[:], True, True))
         wait("V", p_f)
         v_fwu = do(V.tensor_copy(out=T.fwu[:], in_=T.pa[:, 0:128]))
-    else:
-        for r in range(3):
-            pass_on(r)
 
-    vt_ev = {}
+        def count(name):
+            return sum(len(e) for w in workers if w != core for h in range(2) for c, e, n in results_to(w, h)
+                       if c == core and n == name)
 
-    def tokens(h):
-        hs = slice(HALF * h, HALF * h + HALF)
-        lands = {}
-        for i, c in enumerate(ranks):
-            if c == core:
-                lo = 1024 * h + HALF * me
-                lands[c] = T.pk[:, lo:lo + HALF]
-                wait("V", gather_ev[(h, 0)], gather_ev[(h, 1)])
-            else:
-                lands[c] = T.land[:, 128 * i + HALF * h:128 * i + HALF * h + HALF]
-        rwait("V", "toka%d" % h, len([c for c in pair if c != core]))
-        a = do(V.tensor_tensor(out=T.t1[:, hs], in0=lands[pair[0]], in1=lands[pair[1]], op=A.add))
-        rwait("V", "tokb%d" % h, len(other_ranks))
-        b = do(V.tensor_tensor(out=T.t2[:, hs], in0=lands[other_ranks[0]], in1=lands[other_ranks[1]], op=A.add))
-        wait("V", a, b)
-        vt_ev[h] = do(V.tensor_tensor(out=T.vt[:, hs], in0=T.t1[:, hs], in1=T.t2[:, hs], op=A.add))
-
-    groups = [[(0, 0)], [(0, 1)], [(1, 0)], [(1, 1)], [(2, 0), (2, 1)]]
-    seq = [(0, 0), (0, 1), (1, 0), (1, 1), (0, 2), (0, 3), (0, 4), (1, 2), (1, 3), (1, 4)]
-    steps = [(1, 0), (1, 1), (2, 0), (1, 2), (2, 1), (1, 3), (1, 4), (2, 2), (1, 5), (2, 3), (1, 6), (2, 4), (1, 7),
-             (2, 5), (2, 6), (1, 8), (2, 7), (1, 9), (2, 8), (2, 9)]
-    banks = [T.h0, T.h1, T.h2, T.h3]
-    ybank = [T.yp0, T.yp1]
-    relu_ev, y_ev, out_ev, done = {}, {}, {}, [0, 0]
-
-    def tiles(gr):
-        out = []
-        for rs in groups[gr]:
-            col, _, n = reg[rs]
-            out += [(col + 128 * i, col + 128 * n + 128 * i) for i in range(n)]
-        return out
-
-    tokens(0)
-    tokens(1)
-    y_ev[0], y_ev[1] = ev(), ev()
-    for layer, idx in steps:
-        h, gr = seq[idx]
-        ts = tiles(gr)
-        if layer == 1:
-            wait("P", vt_ev[h])
-            for r, s in groups[gr]:
-                need_weights(r, s)
-            e = ev()
-            for m, (ca, _) in enumerate(ts):
-                on(e, P.matmul(banks[idx % 4][:, HALF * m:HALF * m + HALF], T.wt[:, ca:ca + 128],
-                               T.vt[:, HALF * h:HALF * h + HALF], True, True))
-            wait("S", e)
-            relu_ev[idx] = do(S.activation(out=T.hid[:, 512 * idx:512 * idx + HALF * len(ts)],
-                                           in_=banks[idx % 4][:, 0:HALF * len(ts)], func=RELU))
-        else:
-            wait("P", relu_ev[idx])
-            for m, (_, cb) in enumerate(ts):
-                lo = 512 * idx + HALF * m
-                on(y_ev[h], P.matmul(ybank[h][:, 0:HALF], T.wt[:, cb:cb + 128], T.hid[:, lo:lo + HALF],
-                                     done[h] == 0, done[h] == 31))
-                done[h] += 1
-            if done[h] == 32:
-                at = R0 + 1024 * h + HALF * me
-                src = T.win[:, at:at + HALF] if is_rank else T.ys[:, HALF * h:HALF * h + HALF]
-                wait("V", y_ev[h])
-                out_ev[h] = do(V.tensor_copy(out=src, in_=ybank[h][:, 0:HALF]))
-                wait("G", out_ev[h])
-                send([(src, T.win[:, at:at + HALF], [c], eng, "res%d" % h) for c, eng in results_to(core)])
-
-    if is_rank:
+        rwait("G", "resf0", count("resf0"))
+        far = [workers.index(c) for c in workers if topo.chip(c) != chip and topo.die(c) == topo.die(core)]
+        lo, hi = R0 + HALF * min(far), R0 + HALF * (max(far) + 1)
+        send([(T.win[:, lo:hi], T.win[:, lo:hi], [pair[1 - side]], all_eng, "resx")])
         for q in ("V", "S"):
             wait(q, v_fwu, out_ev[0], out_ev[1])
-            for h in range(2):
-                rwait(q, "res%d" % h, sum(len(e) for w in workers if w != core for c, e in results_to(w) if c == core))
+            for n in ("res0", "resf0", "res1"):
+                rwait(q, n, count(n))
+            rwait(q, "resx", len(all_eng))
         yev = ev()
         for k in range(4):
             lo = 512 * k

@@ -8,11 +8,15 @@ X0 = 4
 R0 = X0 + NT
 WIN = R0 + NT
 ZWIN = 8224
-ROUNDS = [6, 6, 4]
+ROUNDS = [4, 4, 4]
 NR = len(ROUNDS)
 EARLY = 2
+MT = 4
+FT = sum(ROUNDS) + MT
+MW = 256 * sum(ROUNDS)
+PIECE = 64 * MT
 HS = 384
-NEV = 130
+NEV = 112
 
 SCRATCH = {
     "wt": ("sbuf", [128, 4096], "float32"),
@@ -69,8 +73,8 @@ SCRATCH = {
     "vt": ("sbuf", [128, 128], "float32"),
     "ys": ("sbuf", [128, 128], "float32"),
     "pv": ("sbuf", [128, 128], "float32"),
-    "pp": ("sbuf", [128, 128], "float32"),
-    "pl": ("sbuf", [128, 128], "float32"),
+    "pp": ("sbuf", [128, 256], "float32"),
+    "pl": ("sbuf", [128, 256], "float32"),
     "h0": ("psum", [128, 512], "float32"),
     "h1": ("psum", [128, 512], "float32"),
     "h2": ("psum", [128, 512], "float32"),
@@ -80,13 +84,14 @@ SCRATCH = {
     "pa": ("psum", [128, 512], "float32"),
     "pb": ("psum", [128, 512], "float32"),
 }
-REMOTE = (["cntin", "sent"] + ["piece%d" % r for r in range(NR)] + ["wr%d" % r for r in range(NR)]
-          + ["%s%d" % (k, h) for k in ("fwd", "par", "toka", "tokb", "res") for h in range(2)] + ["resf0", "resx"])
+REMOTE = (["cntin", "sent", "mpiece", "mcar", "mrel", "mh0", "mh1", "mtp0", "mtn0"]
+          + ["piece%d" % r for r in range(NR)] + ["wr%d" % r for r in range(NR)]
+          + ["%s%d" % (k, h) for k in ("fwd", "par", "mo", "toka", "tokb", "res") for h in range(2)] + ["resf0", "resx"])
 SEMAPHORES = REMOTE + ["e%d" % i for i in range(NEV)]
 
 
 def weight_layout(side):
-    reg, col, f = [], 0, side * sum(ROUNDS)
+    reg, col, f = [], 0, side * FT
     for n in ROUNDS:
         reg.append((col, f, n))
         col += 256 * n
@@ -99,7 +104,7 @@ def pieces(reg, r, eng):
     if r < EARLY:
         to, es = [0, 0, 0, 1, 1, 1, 2, 2], [eng[2 * i:2 * i + 2] for i in range(8)]
     else:
-        to, es = [0, 0, 1, 2], [eng[12:14], eng[14:16], eng[8:12], eng[4:8]]
+        to, es = [0, 0, 1, 2], [eng[10:12], eng[12:14], eng[4:8], eng[8:10]]
     q = 256 * n // len(to)
     return [(i, col + k * q, col + (k + 1) * q, es[k]) for k, i in enumerate(to)]
 
@@ -112,26 +117,107 @@ def mk_mask(bl):
     return sum(1 << i for i in bl)
 
 
+def mate_program(g, core, T, topo, mates8, mate_of, couples):
+    V, S, P = g.vector, g.scalar, g.tensor
+    own = [c for c in mate_of if core in mate_of[c]][0]
+    other = [b if a == own else a for a, b in couples if own in (a, b)][0]
+    h = mate_of[own].index(core)
+    mate = mate_of[own][1 - h]
+    w = PIECE
+    peers = [c for c in mates8 if c != core]
+    every = bits(topo.mask(core, peers[0]))
+    sent = [0]
+
+    def send(src, dst, dests, eng, sem):
+        g.remote_dma_fused([RemoteDMATransfer(
+            srcs=[src], dsts=[dst] * len(dests), dst_ids=[DstId(rid=topo.addr(c)[0], pnc=topo.addr(c)[1]) for c in dests],
+            dma_engine_mask=mk_mask(eng), remote_sem=T.sem[sem])], local_sem=T.sem.sent)
+        sent[0] += len(eng)
+
+    lo = w * mates8.index(core)
+    g.wait_ge(T.sem.mcar, 2)
+    send(T.wt[:, lo:lo + w], T.wt[:, lo:lo + w], peers, every, "mrel")
+    P.wait_ge(T.sem.mcar, 2)
+    P.wait_ge(T.sem.mrel, 7 * len(every))
+    tiles = [(256 * MT * d + 128 * i, 256 * MT * d + 128 * (MT + i)) for d in range(2) for i in range(MT)]
+    nt = len(tiles)
+    hb, yb = [T.h0, T.h1, T.h2, T.h3], [T.yp0, T.yp1]
+    cut = [0, nt // 2, nt]
+    for i, (sem, to, buf) in enumerate([("mtp0", own, T.vt), ("mtn0", other, T.pv)]):
+        P.wait_ge(T.sem[sem], 4 if T.rank_of(own) is not None else len(bits(topo.mask(own, core))))
+        e = [T.sem["e%d" % (6 * i + q)] for q in range(6)]
+        for u in range(2):
+            bank, n, at = hb[2 * i + u], cut[u + 1] - cut[u], 512 * i + HALF * cut[u]
+            for m in range(n):
+                ca = tiles[cut[u] + m][0]
+                P.matmul(bank[:, HALF * m:HALF * m + HALF], T.wt[:, ca:ca + 128], buf[:, 0:HALF], True, True).then_inc(e[u], 1)
+            S.wait_ge(e[u], n)
+            S.activation(out=T.hid[:, at:at + HALF * n], in_=bank[:, 0:HALF * n],
+                         func=ActivationFunctionType.Relu).then_inc(e[2 + u], 1)
+        for u in range(2):
+            P.wait_ge(e[2 + u], 1)
+            for m in range(cut[u], cut[u + 1]):
+                cb, q = tiles[m][1], 512 * i + HALF * m
+                P.matmul(yb[i][:, 0:HALF], T.wt[:, cb:cb + 128], T.hid[:, q:q + HALF], m == 0, m == nt - 1).then_inc(e[4], 1)
+        V.wait_ge(e[4], nt)
+        out = T.land[:, HALF * i:HALF * i + HALF]
+        V.tensor_copy(out=out, in_=yb[i][:, 0:HALF]).then_inc(e[5], 1)
+        back = T.land[:, 128 + HALF * i:192 + HALF * i]
+        if h == 0:
+            g.wait_ge(e[5], 1)
+            send(out, back, [mate], every, "mh%d" % i)
+        else:
+            off = bits(topo.mask(core, own))
+            g.wait_ge(T.sem["mh%d" % i], len(every))
+            send(back, T.pl[:, 128:192], [to], off, "mo0")
+            g.wait_ge(e[5], 1)
+            send(out, T.pl[:, 192:256], [to], off, "mo1")
+    g.wait_ge(T.sem.sent, sent[0])
+
+
 def rank_program(g, core, T, topo):
     ranks = list(T.cores)
     chips = []
     for c in ranks:
         if topo.chip(c) not in chips:
             chips.append(topo.chip(c))
-    if topo.chip(core) not in chips:
+    all_chips = sorted(set(topo.chip(c) for c in range(SIM_CORES)))
+    mates = [[m for m in all_chips if topo.mates(ch, m)][0] for ch in chips]
+    if topo.chip(core) not in chips + mates:
         return
     workers = [c for ch in chips for c in range(SIM_CORES) if topo.chip(c) == ch]
-    me = workers.index(core)
+    me = workers.index(core) if core in workers else None
     rank = T.rank_of(core)
-    chip = topo.chip(core)
-    ck = chips.index(chip)
+    ck = chips.index(topo.chip(core)) if topo.chip(core) in chips else mates.index(topo.chip(core))
+    chip = chips[ck]
     pairs = [[c for c in ranks if topo.chip(c) == ch] for ch in chips]
     pair, other_ranks = pairs[ck], pairs[1 - ck]
     local = [c for c in workers if topo.chip(c) == chip]
     helpers = [[c for c in local if topo.die(c) == topo.die(p) and c not in ranks] for p in pair]
+    dies = [topo.die(p) for p in pair]
+    mates8 = [c for d in dies for c in range(SIM_CORES) if topo.chip(c) == mates[ck] and topo.die(c) == d]
+    backs = [c for c in mates8 if topo.may_write(c, local[0])]
+    owners = [c for d in dies for c in local if topo.may_write(c, mates8[0]) and topo.die(c) == d]
+    mate_of = {a: b for a, b in zip(owners, zip([c for c in mates8 if c not in backs], backs))}
+
+    def fits(a, b):
+        return (a in owners) != (b in owners)
+
+    couples = [(pair[0], [c for c in helpers[1] if fits(c, pair[0])][0]),
+               ([c for c in helpers[0] if fits(c, pair[1])][0], pair[1])]
+    for a in helpers[0]:
+        used = [c for cc in couples for c in cc]
+        if a not in used:
+            couples.append((a, [b for b in helpers[1] if b not in used and fits(a, b)][0]))
+    carrier = [[c for c in hs if c in owners][0] for hs in helpers]
+    if core in mates8:
+        mate_program(g, core, T, topo, mates8, mate_of, couples)
+        return
+    if core not in local:
+        return
     side = [i for i in range(2) if core == pair[i] or core in helpers[i]][0]
-    mine, theirs = [pair[side]] + helpers[side], [pair[1 - side]] + helpers[1 - side]
-    partner = theirs[mine.index(core)]
+    partner = [b if a == core else a for a, b in couples if core in (a, b)][0]
+    owner = core in owners
     reg = weight_layout(side)
     A = AluOpType
     V, S, P, Y = g.vector, g.scalar, g.tensor, g.sync
@@ -198,7 +284,9 @@ def rank_program(g, core, T, topo):
 
     off_eng, stay_eng, all_eng = engines(core)
     is_rank = rank is not None
-    fwd_eng = all_eng[0:4] if is_rank else stay_eng
+    fwd_eng = [stay_eng[-1:], stay_eng[-2:]] if is_rank else [stay_eng] * 2
+    fwd_in = [1, 2] if partner in ranks else [len(stay_eng)] * 2
+    mate_eng = off_eng[0:4] if is_rank else off_eng
     load = {}
     gather_ev = {}
 
@@ -226,12 +314,11 @@ def rank_program(g, core, T, topo):
             q = Y if gq < 4 else S
             on(kev, q.dma_start(T.kp[16 * gq:16 * gq + 16, :], T.keep[:, 16 * gq:16 * gq + 16]), 16)
 
-        def load_round(r, qa, qb):
-            col, f, n = reg[r]
+        def load_tiles(key, col, f, n, qa, qb):
             e = ev()
             on(e, qa.dma_start(T.wt[:, col:col + 128 * n], T.w1[:, 128 * f:128 * (f + n)]), 16)
             on(e, qb.dma_start(T.wt[:, col + 128 * n:col + 256 * n], T.w2[:, 128 * f:128 * (f + n)]), 16)
-            load[r] = e
+            load[key] = e
 
         xev = ev()
 
@@ -239,8 +326,9 @@ def rank_program(g, core, T, topo):
             on(xev, Y.dma_start(T.win[:, X0:X0 + NT // 2], T.x[:, 0:NT // 2]), 16)
             on(xev, Y.dma_start(T.win[:, X0 + NT // 2:R0], T.x[:, NT // 2:NT]), 16)
 
+        load_tiles("m", MW, side * FT + sum(ROUNDS), MT, Y, S)
         for r in range(EARLY):
-            load_round(r, Y, S)
+            load_tiles(r, *reg[r], Y, S)
         if not first:
             load_x()
 
@@ -326,14 +414,20 @@ def rank_program(g, core, T, topo):
             wait("S", v_lu, xev, v_zc)
             gather_ev[(h, 1)] = do(S.activation(out=T.pk[:, 1024 * h + 512:1024 * h + 1024],
                                                 in_=T.win[:, 0:R0].indirect(T.lu[:, 64 * h + 32:64 * h + 64]), func=COPY))
-        wait("Y", p_l[0])
+        wait("Y", gather_ev[(0, 0)])
         for r in range(EARLY, NR):
-            load_round(r, Y, Y)
+            load_tiles(r, *reg[r], Y, Y)
 
         def share(r):
             wait("G", load[r])
             send([(T.wt[:, lo:hi], T.wt[:, lo:hi], [helpers[side][i]], eng, "piece%d" % r)
                   for i, lo, hi, eng in pieces(reg, r, all_eng)])
+
+        def share_mate():
+            wait("G", load["m"])
+            q = 32 * MT
+            send([(T.wt[:, MW + k * q:MW + (k + 1) * q], T.wt[:, MW + k * q:MW + (k + 1) * q], [carrier[side]],
+                   all_eng[2 * k:2 * k + 2], "mpiece") for k in range(8)])
 
         def dispatch(h):
             wait("G", gather_ev[(h, 0)], gather_ev[(h, 1)])
@@ -341,7 +435,8 @@ def rank_program(g, core, T, topo):
             over = [c for c in near if topo.die(c) != topo.die(core)]
             same = [c for c in near if topo.die(c) == topo.die(core)]
             near = [c for i in range(len(over)) for c in [over[i]] + same[i:i + 1]]
-            far = [c for c in workers if topo.chip(c) != chip]
+            far = [c for c in workers if topo.chip(c) != chip and c not in ranks]
+            far = [other_ranks[0], far[0], other_ranks[1]] + far[1:]
             tr = []
             for dests, eng, k in ((far, off_eng, "b"), (near, stay_eng, "a")):
                 for c, b in zip(dests, eng):
@@ -350,13 +445,20 @@ def rank_program(g, core, T, topo):
                     tr.append((T.pk[:, lo:lo + HALF], T.land[:, to:to + HALF], [c], [b], "tok%s%d" % (k, h)))
             send(tr)
 
+        share_mate()
         for r in range(EARLY):
             share(r)
         dispatch(0)
         dispatch(1)
-        for r in range(EARLY, NR):
-            share(r)
     else:
+        if core == carrier[side]:
+            rwait("G", "mpiece", len(all_eng))
+            tr = []
+            for k in range(4):
+                to = 4 * side + k
+                tr.append((T.wt[:, MW + PIECE * k:MW + PIECE * k + PIECE], T.wt[:, PIECE * to:PIECE * to + PIECE],
+                           [mates8[to]], off_eng[2 * k:2 * k + 2], "mcar"))
+            send(tr)
         for r in range(EARLY):
             pass_on(r)
 
@@ -379,8 +481,12 @@ def rank_program(g, core, T, topo):
         wait("V", a, b)
         vt_ev[h] = do(V.tensor_tensor(out=T.vt[:, hs], in0=T.t1[:, hs], in1=T.t2[:, hs], op=A.add))
 
-    seq = [(0, 0, 6), (0, 6, 12), (2, 0, 6), (2, 6, 12), (1, 0, 6), (3, 0, 6), (2, 12, 16), (3, 6, 12), (3, 12, 16),
-           (0, 12, 16), (1, 6, 12), (1, 12, 16)]
+    ta, tb, tc = ROUNDS[0], ROUNDS[0] + ROUNDS[1], sum(ROUNDS)
+    seq = [(0, 0, ta), (0, ta, tb), (2, 0, ta), (2, ta, tb), (1, 0, ta)]
+    if is_rank:
+        seq += [(1, ta, tb), (3, 0, ta), (3, ta, tb), (2, tb, tc), (3, tb, tc), (0, tb, tc), (1, tb, tc)]
+    else:
+        seq += [(3, 0, ta), (3, ta, tb), (2, tb, tc), (3, tb, tc), (0, tb, tc), (1, ta, tb), (1, tb, tc)]
     steps = [(1, 0), (1, 1), (2, 0), (2, 1), (1, 2), (1, 3), (2, 2)]
     for i in range(4, len(seq)):
         steps += [(1, i), (2, i - 2)]
@@ -396,11 +502,24 @@ def rank_program(g, core, T, topo):
     relu_ev, out_ev, pp_ev, done = {}, {}, {}, [0] * 4
     y_ev = [ev() for _ in range(4)]
 
+    def partner_to_mate(h):
+        hs = slice(HALF * h, HALF * h + HALF)
+        rwait("G", "fwd%d" % h, fwd_in[h])
+        send([(T.pv[:, hs], T.pv[:, 0:HALF], [mate_of[core][h]], mate_eng, "mtn0")])
+
     for h in range(2):
         tokens(h)
         wait("G", vt_ev[h])
         hs = slice(HALF * h, HALF * h + HALF)
-        send([(T.vt[:, hs], T.pv[:, hs], [partner], fwd_eng, "fwd%d" % h)])
+        tr = [(T.vt[:, hs], T.pv[:, hs], [partner], fwd_eng[h], "fwd%d" % h)]
+        if owner:
+            tr.append((T.vt[:, hs], T.vt[:, 0:HALF], [mate_of[core][h]], mate_eng, "mtp0"))
+        send(tr)
+        if is_rank and h == 0:
+            for r in range(EARLY, NR):
+                share(r)
+        if owner and h == 0:
+            partner_to_mate(0)
     if is_rank:
         v_k1 = do(V.tensor_copy(out=T.k1[:], in_=T.kp[:]))
         v_q15 = do(V.tensor_scalar(out=T.q15[:, 0:1], in0=T.qi[:, 0:1], scalar1=15, scalar2=None, op0=A.mult))
@@ -431,6 +550,8 @@ def rank_program(g, core, T, topo):
     else:
         for r in range(EARLY, NR):
             pass_on(r)
+    if owner:
+        partner_to_mate(1)
     for layer, idx in steps:
         st, fa, fb = seq[idx]
         h = st % 2
@@ -441,7 +562,7 @@ def rank_program(g, core, T, topo):
             if st < 2:
                 wait("P", vt_ev[h])
             else:
-                rwait("P", "fwd%d" % h, len(all_eng[0:4]) if is_rank else len(stay_eng))
+                rwait("P", "fwd%d" % h, fwd_in[h])
             for r in sorted(set(t[0] for t in tl)):
                 need_weights(r)
             e = ev()
@@ -460,16 +581,20 @@ def rank_program(g, core, T, topo):
             done[st] += 1
         if done[st] < len(tiles):
             continue
-        wait("V", y_ev[st])
         if st >= 2:
+            wait("V", y_ev[st])
             pp_ev[h] = do(V.tensor_copy(out=T.pp[:, hs], in_=ybank[st][:, 0:HALF]))
             wait("G", pp_ev[h])
             send([(T.pp[:, hs], T.pl[:, hs], [partner], all_eng, "par%d" % h)])
         else:
             at = R0 + 1024 * h + HALF * me
             src = T.win[:, at:at + HALF] if is_rank else T.ys[:, hs]
+            ms = slice(128 + HALF * h, 128 + HALF * h + HALF)
             rwait("V", "par%d" % h, len(all_eng))
-            out_ev[h] = do(V.tensor_tensor(out=src, in0=ybank[st][:, 0:HALF], in1=T.pl[:, hs], op=A.add))
+            rwait("V", "mo%d" % h, len(off_eng))
+            pm_ev = do(V.tensor_tensor(out=T.pp[:, ms], in0=T.pl[:, ms], in1=T.pl[:, hs], op=A.add))
+            wait("V", y_ev[st], pm_ev)
+            out_ev[h] = do(V.tensor_tensor(out=src, in0=ybank[st][:, 0:HALF], in1=T.pp[:, ms], op=A.add))
             wait("G", out_ev[h])
             send([(src, T.win[:, at:at + HALF], [c], eng, sem) for c, eng, sem in results_to(core, h)])
 

from concourse.bass import DstId, RemoteDMATransfer
from concourse.mybir import AluOpType, AxisListType, ActivationFunctionType

SIM_CORES = 128
NT = 2048
HALF = 64
X0 = 4
R0 = X0 + NT
WIN = R0 + NT
ZWIN = 8224
ROUNDS = [4, 4, 4]
NR = len(ROUNDS)
EARLY = 2
MT = 4
FT = sum(ROUNDS) + MT
MW = 256 * sum(ROUNDS)
PIECE = 64 * MT
HS = 384
NEV = 112

SCRATCH = {
    "wt": ("sbuf", [128, 4096], "float32"),
    "win": ("sbuf", [128, WIN], "float32"),
    "pk": ("sbuf", [128, NT], "float32"),
    "yo": ("sbuf", [128, NT], "float32"),
    "hid": ("sbuf", [128, 12 * HS], "float32"),
    "zw": ("sbuf", [128, ZWIN], "bfloat16"),
    "hi": ("sbuf", [128, 256], "bfloat16"),
    "lo": ("sbuf", [128, 256], "bfloat16"),
    "hi0": ("sbuf", [128, 256], "bfloat16"),
    "lo1": ("sbuf", [128, 256], "bfloat16"),
    "num": ("sbuf", [128, 256], "bfloat16"),
    "strip": ("sbuf", [128, 144], "bfloat16"),
    "mk": ("sbuf", [128, 128], "int32"),
    "mk15": ("sbuf", [128, 128], "int32"),
    "up": ("sbuf", [128, 128], "float32"),
    "ones": ("sbuf", [128, 128], "float32"),
    "same": ("sbuf", [128, 128], "float32"),
    "fexp": ("sbuf", [128, 128], "float32"),
    "pcol": ("sbuf", [128, 4], "int32"),
    "qi": ("sbuf", [128, 4], "int32"),
    "p4i": ("sbuf", [128, 4], "int32"),
    "m0": ("sbuf", [128, 4], "float32"),
    "m1": ("sbuf", [128, 4], "float32"),
    "q15": ("sbuf", [128, 4], "float32"),
    "p4": ("sbuf", [128, 4], "float32"),
    "cnt": ("sbuf", [128, 4], "float32"),
    "cnta": ("sbuf", [128, 4], "float32"),
    "gi": ("sbuf", [128, 8], "float32"),
    "gm": ("sbuf", [128, 8], "float32"),
    "kp": ("sbuf", [128, 16], "int32"),
    "kf": ("sbuf", [128, 16], "float32"),
    "k1": ("sbuf", [128, 16], "float32"),
    "nk": ("sbuf", [128, 16], "float32"),
    "nkt": ("sbuf", [128, 16], "float32"),
    "zr": ("sbuf", [128, 16], "float32"),
    "tr": ("sbuf", [128, 16], "float32"),
    "incl": ("sbuf", [128, 16], "float32"),
    "gk": ("sbuf", [128, 16], "float32"),
    "t4a": ("sbuf", [128, 16], "float32"),
    "t4": ("sbuf", [128, 16], "float32"),
    "offf": ("sbuf", [128, 16], "float32"),
    "e1": ("sbuf", [128, 16], "float32"),
    "e2": ("sbuf", [128, 16], "float32"),
    "e3": ("sbuf", [128, 16], "float32"),
    "fw": ("sbuf", [128, 16], "float32"),
    "off16": ("sbuf", [128, 16], "uint16"),
    "lu": ("sbuf", [128, 128], "uint16"),
    "fwu": ("sbuf", [128, 128], "uint16"),
    "land": ("sbuf", [128, 512], "float32"),
    "t1": ("sbuf", [128, 128], "float32"),
    "t2": ("sbuf", [128, 128], "float32"),
    "vt": ("sbuf", [128, 128], "float32"),
    "ys": ("sbuf", [128, 128], "float32"),
    "pv": ("sbuf", [128, 128], "float32"),
    "pp": ("sbuf", [128, 256], "float32"),
    "pl": ("sbuf", [128, 256], "float32"),
    "h0": ("psum", [128, 512], "float32"),
    "h1": ("psum", [128, 512], "float32"),
    "h2": ("psum", [128, 512], "float32"),
    "h3": ("psum", [128, 512], "float32"),
    "yp0": ("psum", [128, 512], "float32"),
    "yp1": ("psum", [128, 512], "float32"),
    "pa": ("psum", [128, 512], "float32"),
    "pb": ("psum", [128, 512], "float32"),
}
REMOTE = (["cntin", "sent", "mpiece", "mcar", "mrel", "mh0", "mh1", "mtp0", "mtn0"]
          + ["piece%d" % r for r in range(NR)] + ["wr%d" % r for r in range(NR)]
          + ["%s%d" % (k, h) for k in ("fwd", "par", "mo", "toka", "tokb", "res") for h in range(2)] + ["resf0", "resx"])
SEMAPHORES = REMOTE + ["e%d" % i for i in range(NEV)]


def weight_layout(side):
    reg, col, f = [], 0, side * FT
    for n in ROUNDS:
        reg.append((col, f, n))
        col += 256 * n
        f += n
    return reg


def pieces(reg, r, eng):
    col, _, n = reg[r]
    if r < EARLY:
        to, es = [0, 0, 0, 1, 1, 1, 2, 2], [eng[2 * i:2 * i + 2] for i in range(8)]
    else:
        to, es = [0, 0, 1, 2], [eng[10:12], eng[12:14], eng[4:8], eng[8:10]]
    q = 256 * n // len(to)
    return [(i, col + k * q, col + (k + 1) * q, es[k]) for k, i in enumerate(to)]


def bits(m):
    return [i for i in range(16) if (m >> i) & 1]


def mk_mask(bl):
    return sum(1 << i for i in bl)


def mate_program(g, core, T, topo, mates8, mate_of, couples):
    V, S, P = g.vector, g.scalar, g.tensor
    own = [c for c in mate_of if core in mate_of[c]][0]
    other = [b if a == own else a for a, b in couples if own in (a, b)][0]
    h = mate_of[own].index(core)
    mate = mate_of[own][1 - h]
    w = PIECE
    peers = [c for c in mates8 if c != core]
    every = bits(topo.mask(core, peers[0]))
    sent = [0]

    def send(src, dst, dests, eng, sem):
        g.remote_dma_fused([RemoteDMATransfer(
            srcs=[src], dsts=[dst] * len(dests), dst_ids=[DstId(rid=topo.addr(c)[0], pnc=topo.addr(c)[1]) for c in dests],
            dma_engine_mask=mk_mask(eng), remote_sem=T.sem[sem])], local_sem=T.sem.sent)
        sent[0] += len(eng)

    lo = w * mates8.index(core)
    g.wait_ge(T.sem.mcar, 2)
    send(T.wt[:, lo:lo + w], T.wt[:, lo:lo + w], peers, every, "mrel")
    P.wait_ge(T.sem.mcar, 2)
    P.wait_ge(T.sem.mrel, 7 * len(every))
    tiles = [(256 * MT * d + 128 * i, 256 * MT * d + 128 * (MT + i)) for d in range(2) for i in range(MT)]
    nt = len(tiles)
    hb, yb = [T.h0, T.h1, T.h2, T.h3], [T.yp0, T.yp1]
    cut = [0, nt // 2, nt]
    for i, (sem, to, buf) in enumerate([("mtp0", own, T.vt), ("mtn0", other, T.pv)]):
        P.wait_ge(T.sem[sem], 4 if T.rank_of(own) is not None else len(bits(topo.mask(own, core))))
        e = [T.sem["e%d" % (6 * i + q)] for q in range(6)]
        for u in range(2):
            bank, n, at = hb[2 * i + u], cut[u + 1] - cut[u], 512 * i + HALF * cut[u]
            for m in range(n):
                ca = tiles[cut[u] + m][0]
                P.matmul(bank[:, HALF * m:HALF * m + HALF], T.wt[:, ca:ca + 128], buf[:, 0:HALF], True, True).then_inc(e[u], 1)
            S.wait_ge(e[u], n)
            S.activation(out=T.hid[:, at:at + HALF * n], in_=bank[:, 0:HALF * n],
                         func=ActivationFunctionType.Relu).then_inc(e[2 + u], 1)
        for u in range(2):
            P.wait_ge(e[2 + u], 1)
            for m in range(cut[u], cut[u + 1]):
                cb, q = tiles[m][1], 512 * i + HALF * m
                P.matmul(yb[i][:, 0:HALF], T.wt[:, cb:cb + 128], T.hid[:, q:q + HALF], m == 0, m == nt - 1).then_inc(e[4], 1)
        V.wait_ge(e[4], nt)
        out = T.land[:, HALF * i:HALF * i + HALF]
        V.tensor_copy(out=out, in_=yb[i][:, 0:HALF]).then_inc(e[5], 1)
        back = T.land[:, 128 + HALF * i:192 + HALF * i]
        if h == 0:
            g.wait_ge(e[5], 1)
            send(out, back, [mate], every, "mh%d" % i)
        else:
            off = bits(topo.mask(core, own))
            g.wait_ge(T.sem["mh%d" % i], len(every))
            send(back, T.pl[:, 128:192], [to], off, "mo0")
            g.wait_ge(e[5], 1)
            send(out, T.pl[:, 192:256], [to], off, "mo1")
    g.wait_ge(T.sem.sent, sent[0])


def rank_program(g, core, T, topo):
    ranks = list(T.cores)
    chips = []
    for c in ranks:
        if topo.chip(c) not in chips:
            chips.append(topo.chip(c))
    all_chips = sorted(set(topo.chip(c) for c in range(SIM_CORES)))
    mates = [[m for m in all_chips if topo.mates(ch, m)][0] for ch in chips]
    if topo.chip(core) not in chips + mates:
        return
    workers = [c for ch in chips for c in range(SIM_CORES) if topo.chip(c) == ch]
    me = workers.index(core) if core in workers else None
    rank = T.rank_of(core)
    ck = chips.index(topo.chip(core)) if topo.chip(core) in chips else mates.index(topo.chip(core))
    chip = chips[ck]
    pairs = [[c for c in ranks if topo.chip(c) == ch] for ch in chips]
    pair, other_ranks = pairs[ck], pairs[1 - ck]
    local = [c for c in workers if topo.chip(c) == chip]
    helpers = [[c for c in local if topo.die(c) == topo.die(p) and c not in ranks] for p in pair]
    dies = [topo.die(p) for p in pair]
    mates8 = [c for d in dies for c in range(SIM_CORES) if topo.chip(c) == mates[ck] and topo.die(c) == d]
    backs = [c for c in mates8 if topo.may_write(c, local[0])]
    owners = [c for d in dies for c in local if topo.may_write(c, mates8[0]) and topo.die(c) == d]
    mate_of = {a: b for a, b in zip(owners, zip([c for c in mates8 if c not in backs], backs))}

    def fits(a, b):
        return (a in owners) != (b in owners)

    couples = [(pair[0], [c for c in helpers[1] if fits(c, pair[0])][0]),
               ([c for c in helpers[0] if fits(c, pair[1])][0], pair[1])]
    for a in helpers[0]:
        used = [c for cc in couples for c in cc]
        if a not in used:
            couples.append((a, [b for b in helpers[1] if b not in used and fits(a, b)][0]))
    carrier = [[c for c in hs if c in owners][0] for hs in helpers]
    if core in mates8:
        mate_program(g, core, T, topo, mates8, mate_of, couples)
        return
    if core not in local:
        return
    side = [i for i in range(2) if core == pair[i] or core in helpers[i]][0]
    partner = [b if a == core else a for a, b in couples if core in (a, b)][0]
    owner = core in owners
    reg = weight_layout(side)
    A = AluOpType
    V, S, P, Y = g.vector, g.scalar, g.tensor, g.sync
    RELU, COPY = ActivationFunctionType.Relu, ActivationFunctionType.Copy

    events = []

    def ev():
        e = {"s": T.sem["e%d" % len(events)], "n": 0, "q": []}
        events.append(e)
        return e

    def on(e, ins, n=1):
        ins.then_inc(e["s"], n)
        e["n"] += n
        return e

    def do(ins, n=1):
        return on(ev(), ins, n)

    qs = {"V": V, "S": S, "P": P, "Y": Y, "G": g}

    def wait(q, *es):
        for e in es:
            if q not in e["q"]:
                e["q"].append(q)
                qs[q].wait_ge(e["s"], e["n"])

    waited = {}

    def rwait(q, name, n):
        if n and (q, name) not in waited:
            waited[(q, name)] = n
            qs[q].wait_ge(T.sem[name], n)

    def did(c):
        a = topo.addr(c)
        return DstId(rid=a[0], pnc=a[1])

    sent = [0]

    def send(transfers):
        out = []
        for src, dst, dests, eng, sem in transfers:
            out.append(RemoteDMATransfer(srcs=[src], dsts=[dst] * len(dests), dst_ids=[did(c) for c in dests],
                                         dma_engine_mask=mk_mask(eng), remote_sem=T.sem[sem]))
            sent[0] += len(eng)
        g.remote_dma_fused(out, local_sem=T.sem.sent)

    def engines(c):
        off = bits(topo.mask(c, [d for d in workers if topo.chip(d) != topo.chip(c)][0]))
        allb = bits(topo.mask(c, [d for d in workers if topo.chip(d) == topo.chip(c) and d != c][0]))
        return off, [b for b in allb if b not in off], allb

    def results_to(c, h):
        off, stay, _ = engines(c)
        far = [d for d in ranks if topo.chip(d) != topo.chip(c)]
        if h == 0:
            far = [d for d in far if topo.die(d) == topo.die(c)]
        k = len(off) // len(far)
        out = [(d, off[i * k:(i + 1) * k], "resf0" if h == 0 else "res1") for i, d in enumerate(far)]
        near = [d for d in ranks if topo.chip(d) == topo.chip(c) and d != c]
        return out + [(d, stay[i::len(near)], "res%d" % h) for i, d in enumerate(near)]

    off_eng, stay_eng, all_eng = engines(core)
    is_rank = rank is not None
    fwd_eng = [stay_eng[-1:], stay_eng[-2:]] if is_rank else [stay_eng] * 2
    fwd_in = [1, 2] if partner in ranks else [len(stay_eng)] * 2
    mate_eng = off_eng[0:4] if is_rank else off_eng
    load = {}
    gather_ev = {}

    def part(r):
        ps = [p for p in pieces(reg, r, all_eng) if p[0] == helpers[side].index(core)]
        return ps[0][1], ps[-1][2], sum(len(p[3]) for p in ps)

    def pass_on(r):
        lo, hi, n = part(r)
        rwait("G", "piece%d" % r, n)
        send([(T.wt[:, lo:hi], T.wt[:, lo:hi], [c for c in helpers[side] if c != core], all_eng, "wr%d" % r)])

    def need_weights(r):
        if is_rank:
            wait("P", load[r])
        else:
            rwait("P", "piece%d" % r, part(r)[2])
            rwait("P", "wr%d" % r, 2 * len(all_eng))

    if is_rank:
        first = core == pair[0]
        up = ck == 0
        kev = ev()
        for gq in range(8):
            q = Y if gq < 4 else S
            on(kev, q.dma_start(T.kp[16 * gq:16 * gq + 16, :], T.keep[:, 16 * gq:16 * gq + 16]), 16)

        def load_tiles(key, col, f, n, qa, qb):
            e = ev()
            on(e, qa.dma_start(T.wt[:, col:col + 128 * n], T.w1[:, 128 * f:128 * (f + n)]), 16)
            on(e, qb.dma_start(T.wt[:, col + 128 * n:col + 256 * n], T.w2[:, 128 * f:128 * (f + n)]), 16)
            load[key] = e

        xev = ev()

        def load_x():
            on(xev, Y.dma_start(T.win[:, X0:X0 + NT // 2], T.x[:, 0:NT // 2]), 16)
            on(xev, Y.dma_start(T.win[:, X0 + NT // 2:R0], T.x[:, NT // 2:NT]), 16)

        load_tiles("m", MW, side * FT + sum(ROUNDS), MT, Y, S)
        for r in range(EARLY):
            load_tiles(r, *reg[r], Y, S)
        if not first:
            load_x()

        i_mk = do(g.iota(T.mk[:], [[1, 128]], 0, -1))
        i_p = do(g.iota(T.pcol[:, 0:1], [[1, 1]], 0, 1))
        if up:
            i_tr = do(g.iota(T.tr[:], [[1, 16]], 2064, 32, allow_small_or_imprecise_dtypes=True))
        else:
            i_tr = do(g.iota(T.tr[:], [[-1, 16]], 6160, -32, allow_small_or_imprecise_dtypes=True))
        i_lo = do(g.iota(T.lo[:], [[0, 16], [1, 16]], X0, 0, allow_small_or_imprecise_dtypes=True))
        i_hi = do(g.iota(T.hi[:], [[16, 16], [0, 16]], 0, 16, allow_small_or_imprecise_dtypes=True))
        i_t4 = do(g.iota(T.t4a[:], [[16, 16]], X0, 16, allow_small_or_imprecise_dtypes=True))
        i_gi = do(g.iota(T.gi[:], [[1, 8]], 0, 0, allow_small_or_imprecise_dtypes=True))

        v_zr = do(V.memset(T.zr[:], 0.0))
        if not first:
            v_ones = do(V.memset(T.ones[:], 1.0))
        v_zc = do(V.memset(T.win[:, 0:X0], 0.0))
        v_zw = do(V.memset(T.zw[:, 0:NT], 0.0))
        wait("V", i_mk)
        v_up = do(V.tensor_scalar(out=T.up[:], in0=T.mk[:], scalar1=0, scalar2=None, op0=A.is_gt))
        wait("V", i_p)
        v_qi = do(V.tensor_scalar(out=T.qi[:, 0:1], in0=T.pcol[:, 0:1], scalar1=15, scalar2=None, op0=A.bitwise_and))
        wait("V", v_qi)
        v_m0 = do(V.tensor_scalar(out=T.m0[:, 0:1], in0=T.qi[:, 0:1], scalar1=0, scalar2=None, op0=A.is_equal))
        v_m1 = do(V.tensor_scalar(out=T.m1[:, 0:1], in0=T.qi[:, 0:1], scalar1=1, scalar2=None, op0=A.is_equal))

        wait("V", kev)
        v_kf = do(V.tensor_scalar(out=T.kf[:], in0=T.kp[:], scalar1=1 if up else -1, scalar2=None, op0=A.mult))
        wait("V", v_kf)
        v_cnt = do(V.tensor_reduce(out=T.cnt[:, 0:1], in_=T.kf[:], axis=AxisListType.X, op=A.add))
        v_nk = do(V.tensor_scalar(out=T.nk[:], in0=T.kp[:], scalar1=0, scalar2=None, op0=A.is_equal))
        wait("V", v_zr)
        v_in = do(V.tensor_tensor_scan(out=T.incl[:], data0=T.kf[:], data1=T.zr[:], initial=-1.0 if up else float(NT),
                                       op0=A.add, op1=A.add))
        wait("V", v_nk, i_tr)
        v_nkt = do(V.tensor_tensor(out=T.nkt[:], in0=T.nk[:], in1=T.tr[:], op=A.mult))
        wait("V", v_in, v_nkt)
        v_gk = do(V.tensor_tensor(out=T.gk[:], in0=T.incl[:], in1=T.nkt[:], op=A.add))
        wait("V", i_lo, v_m1)
        v_lh = ev()
        on(v_lh, V.tensor_scalar(out=T.lo1[:], in0=T.lo[:], scalar1=T.m1[:, 0:1], scalar2=None, op0=A.mult))
        v_strip = do(V.tensor_scalar(out=T.strip[:], in0=T.lo[:, 0:144], scalar1=X0 + 15, scalar2=None, op0=A.is_equal))
        wait("V", i_hi, v_m0)
        on(v_lh, V.tensor_scalar(out=T.hi0[:], in0=T.hi[:], scalar1=T.m0[:, 0:1], scalar2=None, op0=A.mult))
        wait("V", v_lh)
        v_num = do(V.tensor_tensor(out=T.num[:], in0=T.hi0[:], in1=T.lo1[:], op=A.add))

        if first:
            wait("Y", v_cnt)
            load_x()
            wait("G", v_cnt)
            send([(T.cnt[:, 0:1], T.cnta[:, 0:1], [pair[1]], all_eng[::2], "cntin")])

        wait("P", v_up, v_cnt)
        if first:
            p_base = do(P.matmul(T.pb[:, 0:1], T.up[:], T.cnt[:, 0:1], True, True))
        else:
            p_base = ev()
            on(p_base, P.matmul(T.pb[:, 0:1], T.up[:], T.cnt[:, 0:1], True, False))
            wait("P", v_ones)
            rwait("P", "cntin", len(all_eng[::2]))
            on(p_base, P.matmul(T.pb[:, 0:1], T.ones[:], T.cnta[:, 0:1], False, True))
        wait("V", v_gk, p_base)
        v_off = do(V.tensor_scalar(out=T.off16[:], in0=T.gk[:], scalar1=T.pb[:, 0:1], scalar2=None, op0=A.add))
        wait("V", v_off, v_num, v_zw)
        v_sc = do(V.tensor_copy(out=T.zw[:, 0:ZWIN].indirect(T.off16[:, 0:16]), in_=T.num[:]))
        wait("P", v_sc, v_strip)
        p_l = []
        for h in range(2):
            bank = T.pa if h == 0 else T.pb
            e = ev()
            for q in range(16):
                lo = 1024 * h + q
                on(e, P.matmul(bank[:, 0:64], T.strip[:, 15 - q:143 - q], T.zw[:, lo:lo + 1009:16], q == 0, q == 15))
            p_l.append(e)
        for h in range(2):
            wait("V", p_l[h])
            v_lu = do(V.tensor_copy(out=T.lu[:, 64 * h:64 * h + 64], in_=(T.pa if h == 0 else T.pb)[:, 0:64]))
            wait("V", v_lu, xev, v_zc)
            gather_ev[(h, 0)] = do(V.tensor_copy(out=T.pk[:, 1024 * h:1024 * h + 512],
                                                 in_=T.win[:, 0:R0].indirect(T.lu[:, 64 * h:64 * h + 32])))
            wait("S", v_lu, xev, v_zc)
            gather_ev[(h, 1)] = do(S.activation(out=T.pk[:, 1024 * h + 512:1024 * h + 1024],
                                                in_=T.win[:, 0:R0].indirect(T.lu[:, 64 * h + 32:64 * h + 64]), func=COPY))
        wait("Y", gather_ev[(0, 0)])
        for r in range(EARLY, NR):
            load_tiles(r, *reg[r], Y, Y)

        def share(r):
            wait("G", load[r])
            send([(T.wt[:, lo:hi], T.wt[:, lo:hi], [helpers[side][i]], eng, "piece%d" % r)
                  for i, lo, hi, eng in pieces(reg, r, all_eng)])

        def share_mate():
            wait("G", load["m"])
            q = 32 * MT
            send([(T.wt[:, MW + k * q:MW + (k + 1) * q], T.wt[:, MW + k * q:MW + (k + 1) * q], [carrier[side]],
                   all_eng[2 * k:2 * k + 2], "mpiece") for k in range(8)])

        def dispatch(h):
            wait("G", gather_ev[(h, 0)], gather_ev[(h, 1)])
            near = [c for c in local if c != core]
            over = [c for c in near if topo.die(c) != topo.die(core)]
            same = [c for c in near if topo.die(c) == topo.die(core)]
            near = [c for i in range(len(over)) for c in [over[i]] + same[i:i + 1]]
            far = [c for c in workers if topo.chip(c) != chip and c not in ranks]
            far = [other_ranks[0], far[0], other_ranks[1]] + far[1:]
            tr = []
            for dests, eng, k in ((far, off_eng, "b"), (near, stay_eng, "a")):
                for c, b in zip(dests, eng):
                    lo = 1024 * h + HALF * workers.index(c)
                    to = 128 * rank + HALF * h
                    tr.append((T.pk[:, lo:lo + HALF], T.land[:, to:to + HALF], [c], [b], "tok%s%d" % (k, h)))
            send(tr)

        share_mate()
        for r in range(EARLY):
            share(r)
        dispatch(0)
        dispatch(1)
    else:
        if core == carrier[side]:
            rwait("G", "mpiece", len(all_eng))
            tr = []
            for k in range(4):
                to = 4 * side + k
                tr.append((T.wt[:, MW + PIECE * k:MW + PIECE * k + PIECE], T.wt[:, PIECE * to:PIECE * to + PIECE],
                           [mates8[to]], off_eng[2 * k:2 * k + 2], "mcar"))
            send(tr)
        for r in range(EARLY):
            pass_on(r)

    vt_ev = {}

    def tokens(h):
        hs = slice(HALF * h, HALF * h + HALF)
        lands = {}
        for i, c in enumerate(ranks):
            if c == core:
                lo = 1024 * h + HALF * me
                lands[c] = T.pk[:, lo:lo + HALF]
                wait("V", gather_ev[(h, 0)], gather_ev[(h, 1)])
            else:
                lands[c] = T.land[:, 128 * i + HALF * h:128 * i + HALF * h + HALF]
        rwait("V", "toka%d" % h, len([c for c in pair if c != core]))
        a = do(V.tensor_tensor(out=T.t1[:, hs], in0=lands[pair[0]], in1=lands[pair[1]], op=A.add))
        rwait("V", "tokb%d" % h, len(other_ranks))
        b = do(V.tensor_tensor(out=T.t2[:, hs], in0=lands[other_ranks[0]], in1=lands[other_ranks[1]], op=A.add))
        wait("V", a, b)
        vt_ev[h] = do(V.tensor_tensor(out=T.vt[:, hs], in0=T.t1[:, hs], in1=T.t2[:, hs], op=A.add))

    ta, tb, tc = ROUNDS[0], ROUNDS[0] + ROUNDS[1], sum(ROUNDS)
    seq = [(0, 0, ta), (0, ta, tb), (2, 0, ta), (2, ta, tb), (1, 0, ta)]
    if is_rank:
        seq += [(1, ta, tb), (3, 0, ta), (3, ta, tb), (2, tb, tc), (3, tb, tc), (0, tb, tc), (1, tb, tc)]
    else:
        seq += [(3, 0, ta), (3, ta, tb), (2, tb, tc), (3, tb, tc), (0, tb, tc), (1, ta, tb), (1, tb, tc)]
    steps = [(1, 0), (1, 1), (2, 0), (2, 1), (1, 2), (1, 3), (2, 2)]
    for i in range(4, len(seq)):
        steps += [(1, i), (2, i - 2)]
        if seq[i - 1][0] not in [q[0] for q in seq[i:]]:
            steps.append((2, i - 1))
    steps += [(2, i) for i in range(len(seq))]
    steps = [st for i, st in enumerate(steps) if st not in steps[:i]]
    tiles = []
    for r, (col, f, n) in enumerate(reg):
        tiles += [(r, col + 128 * i, col + 128 * (n + i)) for i in range(n)]
    banks = [T.h0, T.h1, T.h2, T.h3]
    ybank = [T.yp0, T.yp1, T.pa, T.pb]
    relu_ev, out_ev, pp_ev, done = {}, {}, {}, [0] * 4
    y_ev = [ev() for _ in range(4)]

    def partner_to_mate(h):
        hs = slice(HALF * h, HALF * h + HALF)
        rwait("G", "fwd%d" % h, fwd_in[h])
        send([(T.pv[:, hs], T.pv[:, 0:HALF], [mate_of[core][h]], mate_eng, "mtn0")])

    for h in range(2):
        tokens(h)
        wait("G", vt_ev[h])
        hs = slice(HALF * h, HALF * h + HALF)
        tr = [(T.vt[:, hs], T.pv[:, hs], [partner], fwd_eng[h], "fwd%d" % h)]
        if owner:
            tr.append((T.vt[:, hs], T.vt[:, 0:HALF], [mate_of[core][h]], mate_eng, "mtp0"))
        send(tr)
        if is_rank and h == 0:
            for r in range(EARLY, NR):
                share(r)
        if owner and h == 0:
            partner_to_mate(0)
    if is_rank:
        v_k1 = do(V.tensor_copy(out=T.k1[:], in_=T.kp[:]))
        v_q15 = do(V.tensor_scalar(out=T.q15[:, 0:1], in0=T.qi[:, 0:1], scalar1=15, scalar2=None, op0=A.mult))
        v_of = do(V.tensor_copy(out=T.offf[:], in_=T.off16[:]))
        v_p4i = do(V.tensor_scalar(out=T.p4i[:, 0:1], in0=T.pcol[:, 0:1], scalar1=4, scalar2=None, op0=A.arith_shift_right))
        v_mk15 = do(V.tensor_scalar(out=T.mk15[:], in0=T.mk[:], scalar1=15, scalar2=None, op0=A.bitwise_and))
        wait("V", i_t4, v_q15)
        v_t4 = do(V.tensor_scalar(out=T.t4[:], in0=T.t4a[:], scalar1=T.q15[:, 0:1], scalar2=None, op0=A.subtract))
        wait("V", v_p4i)
        v_p4 = do(V.tensor_copy(out=T.p4[:, 0:1], in_=T.p4i[:, 0:1]))
        wait("V", v_mk15)
        v_same = do(V.tensor_scalar(out=T.same[:], in0=T.mk15[:], scalar1=0, scalar2=None, op0=A.is_equal))
        wait("V", v_of, v_t4)
        v_e1 = do(V.tensor_tensor(out=T.e1[:], in0=T.offf[:], in1=T.t4[:], op=A.subtract))
        wait("V", i_gi, v_p4)
        v_gm = do(V.tensor_scalar(out=T.gm[:], in0=T.gi[:], scalar1=T.p4[:, 0:1], scalar2=None, op0=A.is_equal))
        wait("V", v_e1)
        v_e2 = do(V.tensor_scalar(out=T.e2[:], in0=T.e1[:], scalar1=float(R0), scalar2=None, op0=A.add))
        wait("V", v_e2, v_k1)
        v_e3 = do(V.tensor_tensor(out=T.e3[:], in0=T.e2[:], in1=T.k1[:], op=A.mult))
        wait("V", v_e3)
        v_fw = do(V.tensor_tensor(out=T.fw[:], in0=T.e3[:], in1=T.t4[:], op=A.add))
        wait("V", v_fw, v_gm)
        v_fe = ev()
        for k in range(8):
            on(v_fe, V.tensor_scalar(out=T.fexp[:, 16 * k:16 * k + 16], in0=T.fw[:], scalar1=T.gm[:, k:k + 1], scalar2=None,
                                     op0=A.mult))
    else:
        for r in range(EARLY, NR):
            pass_on(r)
    if owner:
        partner_to_mate(1)
    for layer, idx in steps:
        st, fa, fb = seq[idx]
        h = st % 2
        hs = slice(HALF * h, HALF * h + HALF)
        tl = tiles[fa:fb]
        n = len(tl)
        if layer == 1:
            if st < 2:
                wait("P", vt_ev[h])
            else:
                rwait("P", "fwd%d" % h, fwd_in[h])
            for r in sorted(set(t[0] for t in tl)):
                need_weights(r)
            e = ev()
            for m, (_, ca, _) in enumerate(tl):
                on(e, P.matmul(banks[idx % 4][:, HALF * m:HALF * m + HALF], T.wt[:, ca:ca + 128],
                               T.vt[:, hs] if st < 2 else T.pv[:, hs], True, True))
            wait("S", e)
            relu_ev[idx] = do(S.activation(out=T.hid[:, HS * idx:HS * idx + HALF * n],
                                           in_=banks[idx % 4][:, 0:HALF * n], func=RELU))
            continue
        wait("P", relu_ev[idx])
        for m, (_, _, cb) in enumerate(tl):
            lo = HS * idx + HALF * m
            on(y_ev[st], P.matmul(ybank[st][:, 0:HALF], T.wt[:, cb:cb + 128], T.hid[:, lo:lo + HALF],
                                  done[st] == 0, done[st] == len(tiles) - 1))
            done[st] += 1
        if done[st] < len(tiles):
            continue
        if st >= 2:
            wait("V", y_ev[st])
            pp_ev[h] = do(V.tensor_copy(out=T.pp[:, hs], in_=ybank[st][:, 0:HALF]))
            wait("G", pp_ev[h])
            send([(T.pp[:, hs], T.pl[:, hs], [partner], all_eng, "par%d" % h)])
        else:
            at = R0 + 1024 * h + HALF * me
            src = T.win[:, at:at + HALF] if is_rank else T.ys[:, hs]
            ms = slice(128 + HALF * h, 128 + HALF * h + HALF)
            rwait("V", "par%d" % h, len(all_eng))
            rwait("V", "mo%d" % h, len(off_eng))
            pm_ev = do(V.tensor_tensor(out=T.pp[:, ms], in0=T.pl[:, ms], in1=T.pl[:, hs], op=A.add))
            wait("V", y_ev[st], pm_ev)
            out_ev[h] = do(V.tensor_tensor(out=src, in0=ybank[st][:, 0:HALF], in1=T.pp[:, ms], op=A.add))
            wait("G", out_ev[h])
            send([(src, T.win[:, at:at + HALF], [c], eng, sem) for c, eng, sem in results_to(core, h)])

    if is_rank:
        wait("P", v_same, v_fe, pp_ev[0])
        p_f = do(P.matmul(T.pa[:, 0:128], T.same[:], T.fexp[:], True, True))
        wait("V", p_f)
        v_fwu = do(V.tensor_copy(out=T.fwu[:], in_=T.pa[:, 0:128]))

        def count(name):
            return sum(len(e) for w in workers if w != core for h in range(2) for c, e, n in results_to(w, h)
                       if c == core and n == name)

        rwait("G", "resf0", count("resf0"))
        far = [workers.index(c) for c in workers if topo.chip(c) != chip and topo.die(c) == topo.die(core)]
        lo, hi = R0 + HALF * min(far), R0 + HALF * (max(far) + 1)
        send([(T.win[:, lo:hi], T.win[:, lo:hi], [pair[1 - side]], all_eng, "resx")])
        for q in ("V", "S"):
            wait(q, v_fwu, out_ev[0], out_ev[1])
            for n in ("res0", "resf0", "res1"):
                rwait(q, n, count(n))
            rwait(q, "resx", len(all_eng))
        yev = ev()
        for k in range(4):
            lo = 512 * k
            a = do(V.tensor_copy(out=T.yo[:, lo:lo + 256], in_=T.win[:, 0:WIN].indirect(T.fwu[:, 32 * k:32 * k + 16])))
            b = do(S.activation(out=T.yo[:, lo + 256:lo + 512],
                                in_=T.win[:, 0:WIN].indirect(T.fwu[:, 32 * k + 16:32 * k + 32]), func=COPY))
            wait("Y", a, b)
            on(yev, Y.dma_start(T.y[:, lo:lo + 512], T.yo[:, lo:lo + 512]), 16)
        wait("Y", yev)
    g.wait_ge(T.sem.sent, sent[0])
    for e in events:
        if e["n"] and not e["q"]:
            wait("G", e)
